import numpy as np
import ml_dtypes


def mxq(x, axis, fmt="e4m3"):
    dtype, down = {"e4m3": (ml_dtypes.float8_e4m3fn, 7), "e5m2": (ml_dtypes.float8_e5m2, 14)}[fmt]
    v = np.moveaxis(np.asarray(x, np.float32).astype(ml_dtypes.bfloat16).astype(np.float64), axis, -1)
    blocks = v.reshape(v.shape[:-1] + (-1, 32))
    amax = np.abs(blocks).max(-1, keepdims=True)
    byte = np.maximum(np.where(amax > 0, np.frexp(amax)[1] - 1 + 127, 0) - down, 1)
    scale = np.exp2(byte - 127.0)
    codes = (blocks / scale).astype(np.float32).astype(dtype).astype(np.float64)
    return np.moveaxis((codes * scale).reshape(v.shape), -1, axis)


WIDE = False


def mx_kscale(k):
    if not WIDE:
        return np.ones(k)
    levels = np.array([10, -10, 5, -5, 0])
    if k % 512:
        return np.exp2(np.random.permutation(np.resize(levels, k // 32))).repeat(32)
    a = np.empty((k // 512, 16))
    for p in range(k // 512):
        a[p, :8] = np.random.permutation(np.resize(levels, 8))
        for g in range(8):
            far = levels[np.abs(levels - a[p, g]) >= 10]
            a[p, g + 8] = far[np.random.randint(len(far))]
    return np.exp2(a.ravel()).repeat(32)


BF16 = ml_dtypes.bfloat16


def bf(x):
    return np.asarray(x, np.float32).astype(BF16)


def f64(x):
    return np.asarray(x).astype(np.float64)


M, D = 2048, 512


def setup_inputs():
    s, t, u = mx_kscale(D), mx_kscale(D), mx_kscale(M)
    maps = []
    for n in (D, M, D):
        r = np.random.permutation(n)
        e = np.where(np.random.standard_normal(n) > 0, 1.0, -1.0)
        angle = 2 * np.pi / n * (r[:, None] * r)
        reflection = e[:, None] * (np.cos(angle) + np.sin(angle)) / np.sqrt(n) * e
        projector = (np.eye(n) + reflection) / 2
        maps.append(projector * (0.5 + 0.05 * np.random.standard_normal(n)))
    p1, p2, p3 = maps
    return {"x": bf(np.random.standard_normal((M, D)) * s * u[:, None]),
            "p1": bf(p1 / s[:, None] * t),
            "p2": bf(p2 / u[:, None]),
            "p3": bf(p3 / t[:, None]),
            "g1": bf((1 + 0.1 * np.random.standard_normal(D)) * t / s),
            "g2": bf((1 + 0.1 * np.random.standard_normal(M)) / u),
            "g3": bf((1 + 0.1 * np.random.standard_normal(D)) / t)}


def reference(x, p1, p2, p3, g1, g2, g3):
    x = f64(x)
    c1 = mxq(x, 1, "e4m3") @ mxq(f64(p1), 0, "e4m3")
    x1 = x * f64(g1) - c1
    c2 = mxq(f64(p2), 0, "e4m3").T @ mxq(x1, 0, "e4m3")
    x2 = x1 * f64(g2)[:, None] - c2
    c3 = mxq(x2, 1, "e4m3") @ mxq(f64(p3), 0, "e4m3")
    return x2 * f64(g3) - c3

@@ -1,0 +1,385 @@
+from contextlib import ExitStack
+
+import concourse.mybir as mybir
+from concourse.masks import make_identity
+
+M, D = 2048, 512
+FLOPS = 2 * M * D * D + 2 * M * M * D + 2 * M * D * D
+
+F32 = mybir.dt.float32
+BF16 = mybir.dt.bfloat16
+U32 = mybir.dt.uint32
+U8 = mybir.dt.uint8
+FP8X4 = mybir.dt.float8_e4m3fn_x4
+MULT = mybir.AluOpType.mult
+ADD = mybir.AluOpType.add
+SUBTRACT = mybir.AluOpType.subtract
+
+P = 128
+PACK = 4
+W = 512
+HALF = W // 2
+GROUPS = M // W
+POOL_COLS = 784
+
+
+def tile_gated_relaxed_block_projections_t1_kernel(tc, x, p1, p2, p3, g1, g2, g3, out):
+    nc = tc.nc
+    with ExitStack() as ctx:
+        sb = ctx.enter_context(tc.tile_pool(name="sb", bufs=1))
+        ps = ctx.enter_context(tc.psum_pool(name="ps", bufs=1))
+        ctx.enter_context(tc.manual_schedule())
+
+        def sbuf(tag, bufs, shape, dtype):
+            return sb.tile(shape, dtype, name=tag, tag=tag, bufs=bufs, align_bytes=64)
+
+        def bank(b):
+            return ps.tile([P, W], F32, name="bank%d" % b, tag="bank%d" % b)
+
+        def quantise(src, tag, bufs):
+            words = src.shape[1] // PACK
+            codes = sbuf(tag + "_codes", bufs, [P, words], U32)
+            scales = sbuf(tag + "_scales", bufs, [P, words], U8)
+            nc.vector.quantize_mx(out=codes[:].bitcast(FP8X4), scales=scales[:], in_=src)
+            return codes, scales
+
+        def mx_pass(acc, stat, s, mov, first_col, start, stop):
+            cols = slice(P * s, P * (s + 1))
+            span = slice(first_col, first_col + acc.shape[1])
+            nc.tensor.matmul_mx(
+                out=acc,
+                lhsT=stat[0][:, cols].bitcast(FP8X4),
+                lhsT_scale=stat[1][:, cols],
+                rhs=mov[0][:, span].bitcast(FP8X4),
+                rhs_scale=mov[1][:, span],
+                start=start,
+                stop=stop,
+            )
+
+        g1_sb = sbuf("g1", 1, [P, PACK], BF16)
+        g3_sb = sbuf("g3", 1, [P, PACK], BF16)
+        g2_sb = sbuf("g2", 1, [P, GROUPS, PACK], BF16)
+        nc.scalar.dma_start(out=g1_sb[:], in_=g1.rearrange("(p s) -> p s", s=PACK))
+
+        x_rows = x.rearrange("(g p t) d -> g p t d", p=P, t=PACK)
+        out_rows = out.rearrange("(g p t) d -> g t p d", p=P, t=PACK)
+        x_raw = {}
+        raw = {}
+
+        def load_x(g, h):
+            half = sbuf("half", 8, [P, 2 * D], BF16)
+            nc.sync.dma_start(out=half[:].rearrange("p (t d) -> p t d", t=2), in_=x_rows[g, :, 2 * h : 2 * h + 2, :])
+            x_raw[g, h] = half
+
+        def load_rows(key, rows):
+            piece = sbuf("raw", 14, [P, PACK, rows.shape[1]], BF16)
+            nc.sync.dma_start(out=piece[:], in_=rows.rearrange("(p j) c -> p j c", j=PACK))
+            raw[key] = piece
+
+        def load_p2(i):
+            n, kk = divmod(i, 2)
+            for k in (2 * kk, 2 * kk + 1):
+                load_rows((n, k), p2[W * k : W * (k + 1), W * n : W * (n + 1)])
+
+        load_x(0, 0)
+        load_rows(("p1", 0), p1[:, :HALF])
+        load_rows(("p1", 1), p1[:, HALF:])
+        load_x(0, 1)
+        load_x(1, 0)
+        load_x(1, 1)
+        load_rows(("p3", 0), p3[:, :HALF])
+        load_rows(("p3", 1), p3[:, HALF:])
+        nc.sync.dma_start(out=g2_sb[:], in_=g2.rearrange("(g p t) -> p g t", p=P, t=PACK))
+        load_x(2, 0)
+        load_x(2, 1)
+        load_p2(0)
+        load_x(3, 0)
+        load_x(3, 1)
+        load_p2(2)
+        load_p2(1)
+        nc.sync.dma_start(out=g3_sb[:], in_=g3.rearrange("(p s) -> p s", s=PACK))
+        load_p2(3)
+        load_p2(5)
+
+        ident = sbuf("ident", 1, [P, P], F32)
+        make_identity(nc, ident[:])
+        g2_f32 = sbuf("g2_f32", 1, [P, GROUPS * PACK], F32)
+        nc.gpsimd.tensor_copy(out=g2_f32[:], in_=g2_sb[:].rearrange("p g t -> p (g t)"))
+
+        xt = {}
+        xq = {}
+        run = {}
+        x1b = {}
+        x1q = {}
+        stage = {}
+        p2q = {}
+        x2b = {}
+        x2q = {}
+        yt = {}
+        acc1 = {}
+        acc2 = {}
+        acc3 = {}
+        g2_bank = {}
+        turned = {}
+        MM_BANKS = (2, 3, 4, 6)
+        Y_BANKS = (5, 0, 1, 7)
+
+        def turn_x(g, h, b):
+            if h == 0:
+                xt[g] = sbuf("wide", 4, [P, PACK * W], BF16)
+                run[g] = sbuf("run", 4, [P, PACK, W], F32)
+            words = x_raw[g, h][:].bitcast(F32)
+            bk = bank(b)
+            for t in range(2):
+                for u in range(2):
+                    first = 256 * t + u
+                    nc.tensor.transpose(bk[:, P * (2 * t + u) : P * (2 * t + u + 1)], words[:, first : 256 * (t + 1) : 2], ident[:])
+            dst = xt[g][:].bitcast(F32)[:, W * h : W * (h + 1)]
+            nc.scalar.copy(out=dst.rearrange("p (t r u) -> p t r u", t=2, u=2), in_=bk[:].rearrange("p (t u r) -> p t r u", t=2, u=2))
+
+        def regroup_weight(copy, grouped, key, h):
+            dst = grouped[:].rearrange("p (s a b j) -> p a s b j", s=PACK, b=2, j=PACK)
+            src = raw[key, h][:].rearrange("p j (a b s) -> p a s b j", s=PACK, b=2)
+            copy(out=dst[:, 32 * h : 32 * (h + 1)], in_=src)
+
+        def project1(g, s):
+            acc1[g, s] = bank(MM_BANKS[s])[:]
+            mx_pass(acc1[g, s], p1q, s, xq[g], 0, True, True)
+
+        def project_half(accs, weight, operand, first_bank):
+            for pair in range(2):
+                bk = bank(MM_BANKS[first_bank + pair])
+                for s in (2 * pair, 2 * pair + 1):
+                    accs[s] = bk[:, HALF * (s % 2) : HALF * (s % 2 + 1)]
+                    mx_pass(accs[s], weight, s, operand, 0, True, True)
+
+        def gate1(g, s, acc, lo, hi):
+            nc.vector.scalar_tensor_tensor(
+                out=run[g][:, s, lo:hi],
+                in0=xt[g][:].rearrange("p (n j) -> p n j", j=PACK)[:, lo:hi, s],
+                scalar=g1_sb[:, s : s + 1],
+                in1=acc,
+                op0=MULT,
+                op1=SUBTRACT,
+            )
+
+        def turn_x1(g, s, b):
+            if s == 0:
+                x1b[g] = sbuf("x1b", 2, [P, PACK * W], BF16)
+            bk = bank(b)
+            for t in range(PACK):
+                nc.tensor.transpose(bk[:, P * t : P * (t + 1)], run[g][:, s, P * t : P * (t + 1)], ident[:])
+            dst = x1b[g][:, W * s : W * (s + 1)]
+            nc.scalar.copy(out=dst.rearrange("p (f t) -> p f t", t=PACK), in_=bk[:].rearrange("p (t f) -> p f t", t=PACK))
+
+        def spread_g2(g):
+            g2_bank[g] = bank(7)
+            for t in range(PACK):
+                col = PACK * g + t
+                nc.tensor.transpose(g2_bank[g][:, P * t : P * (t + 1)], g2_f32[:, col : col + 1].to_broadcast([P, P]), ident[:])
+
+        def gate2(g):
+            for s in range(PACK):
+                nc.vector.tensor_tensor(out=run[g][:, s, :], in0=run[g][:, s, :], in1=g2_bank[g][:], op=MULT)
+
+        def stage_views(i, lo, hi):
+            n, kk = divmod(i, 2)
+            k, c0 = divmod(lo, W)
+            src = raw[n, 2 * kk + k][:, :, c0 : c0 + hi - lo]
+            return stage[i][:, PACK * lo : PACK * hi], src
+
+        def weave_scalar(i, lo, hi):
+            dst, src = stage_views(i, lo, hi)
+            nc.scalar.copy(out=dst.rearrange("p (c i j) -> p c j i", i=4, j=PACK), in_=src.rearrange("p j (c i) -> p c j i", i=4))
+
+        def weave_pool(i, lo, hi):
+            dst, src = stage_views(i, lo, hi)
+            nc.gpsimd.tensor_scalar(
+                out=dst.rearrange("p (c j) -> p c j", j=PACK),
+                in0=src.rearrange("p j c -> p c j"),
+                scalar1=1.0,
+                scalar2=0.0,
+                op0=MULT,
+                op1=ADD,
+            )
+
+        def weave_shared(i):
+            stage[i] = sbuf("stage_shared", 1, [P, 2 * PACK * W], BF16)
+            weave_pool(i, 0, W)
+            weave_pool(i, W, POOL_COLS)
+            weave_scalar(i, POOL_COLS, 2 * W)
+
+        def weave_quarter(i, q):
+            if q == 0:
+                stage[i] = sbuf("stage_scalar", 2, [P, 2 * PACK * W], BF16)
+            weave_scalar(i, 256 * q, 256 * (q + 1))
+
+        def quantise_p2(i):
+            p2q[i] = quantise(stage[i][:], "p2", 8)
+
+        def project2(n, s, ks):
+            for k in ks:
+                if k == 0:
+                    acc2[n, s] = bank(MM_BANKS[s])
+                mx_pass(acc2[n, s][:], x1q[k], s, p2q[2 * n + k // 2], W * (k % 2), k == 0, k == GROUPS - 1)
+
+        def subtract2(n, s, t0, t1):
+            rows = run[n][:, s, :].rearrange("q (t p) -> q t p", t=PACK)[:, t0:t1]
+            acc = acc2[n, s][:].rearrange("q (p t) -> q t p", t=PACK)[:, t0:t1]
+            nc.vector.tensor_tensor(out=rows, in0=rows, in1=acc, op=SUBTRACT)
+
+        def weave_x2(copy, n, lo, hi):
+            woven = sbuf("wide", 4, [P, PACK * (hi - lo)], BF16)
+            copy(
+                out=woven[:].rearrange("p (c i s) -> p c s i", i=4, s=PACK),
+                in_=run[n][:, :, lo:hi].rearrange("p s (c i) -> p c s i", i=4),
+            )
+            return woven
+
+        def project3(n, s, b):
+            acc3[n, s] = bank(b)[:]
+            mx_pass(acc3[n, s], p3q, s, x2q[n], 0, True, True)
+
+        def gate3(n, s, acc, lo, hi):
+            if lo == 0:
+                yt[n, s] = sbuf("half", 8, [P, W], F32)
+            nc.vector.scalar_tensor_tensor(
+                out=yt[n, s][:, lo:hi], in0=run[n][:, s, lo:hi], scalar=g3_sb[:, s : s + 1], in1=acc, op0=MULT, op1=SUBTRACT
+            )
+
+        def turn_y(n, t, b):
+            turned[n, t] = bank(b)
+            for s in range(PACK):
+                nc.tensor.transpose(turned[n, t][:, P * s : P * (s + 1)], yt[n, s][:, P * t : P * (t + 1)], ident[:])
+
+        def store_y(n, t, copy):
+            rows = sbuf("rows", 4, [P, W], F32)
+            copy(out=rows[:].rearrange("p (f s) -> p f s", s=PACK), in_=turned[n, t][:].rearrange("p (s f) -> p f s", s=PACK))
+            nc.sync.dma_start(out=out_rows[n, t], in_=rows[:])
+
+        turn_x(0, 0, 0)
+        p1g = sbuf("grouped", 1, [P, PACK * W], BF16)
+        regroup_weight(nc.vector.tensor_copy, p1g, "p1", 0)
+        regroup_weight(nc.vector.tensor_copy, p1g, "p1", 1)
+        early = quantise(xt[0][:, : PACK * HALF], "x", 3)
+        p1q = quantise(p1g[:], "p1", 1)
+        turn_x(0, 1, 1)
+        acc_early = {}
+        acc_late = {}
+        project_half(acc_early, p1q, early, 0)
+        p3g = sbuf("stage_shared", 1, [P, PACK * W], BF16)
+        regroup_weight(nc.scalar.copy, p3g, "p3", 0)
+        regroup_weight(nc.scalar.copy, p3g, "p3", 1)
+        turn_x(1, 0, 0)
+        late = quantise(xt[0][:, PACK * HALF :], "x", 3)
+        project_half(acc_late, p1q, late, 2)
+        turn_x(1, 1, 1)
+        for s in range(PACK):
+            gate1(0, s, acc_early[s], 0, HALF)
+        for s in range(PACK):
+            gate1(0, s, acc_late[s], HALF, W)
+        xq[1] = quantise(xt[1][:], "x", 3)
+        p3q = quantise(p3g[:], "p3", 1)
+        turn_x1(0, 0, 5)
+        turn_x1(0, 1, 0)
+        for s in range(PACK):
+            project1(1, s)
+        turn_x1(0, 2, 1)
+        turn_x1(0, 3, 5)
+        spread_g2(0)
+
+        for g in range(1, GROUPS):
+            weave_shared((0, 1, 3)[g - 1])
+            if g == 2:
+                load_p2(4)
+            if g == 3:
+                load_p2(6)
+            if g + 1 < GROUPS:
+                turn_x(g + 1, 0, 0)
+                turn_x(g + 1, 1, 1)
+            for s in range(PACK):
+                gate1(g, s, acc1[g, s], 0, W)
+                turn_x1(g, s, (5, 0, 1, 5)[s])
+            gate2(g - 1)
+            if g == GROUPS - 1:
+                for s in range(PACK):
+                    project2(0, s, (0, 1, 2))
+            spread_g2(g)
+            if g < GROUPS - 1:
+                weave_quarter(2, 2 * g - 2)
+                weave_quarter(2, 2 * g - 1)
+                xq[g + 1] = quantise(xt[g + 1][:], "x", 3)
+                for s in range(PACK):
+                    project1(g + 1, s)
+            else:
+                weave_quarter(5, 0)
+                weave_quarter(5, 1)
+            if g < GROUPS - 1:
+                x1q[g - 1] = quantise(x1b[g - 1][:], "x1", 4)
+            if g > 1:
+                x1q[g] = quantise(x1b[g][:], "x1", 4)
+            if g == GROUPS - 1:
+                for s in range(PACK):
+                    project2(0, s, (3,))
+                quantise_p2(2)
+            quantise_p2((0, 1, 3)[g - 1])
+
+        load_p2(7)
+        last = GROUPS - 1
+        for n in range(last):
+            weave_shared((4, 6, 7)[n])
+            for s in range(PACK):
+                subtract2(n, s, 0, PACK)
+            woven = weave_x2(nc.scalar.copy, n, 0, W)
+            project2(n + 1, 0, (0, 1))
+            project2(n + 1, 1, (0, 1))
+            if n == 0:
+                weave_quarter(5, 2)
+                weave_quarter(5, 3)
+                gate2(last)
+            else:
+                for s in range(PACK):
+                    gate3(n - 1, s, acc3[n - 1, s], 0, W)
+            project2(n + 1, 2, (0, 1))
+            project2(n + 1, 3, (0, 1))
+            if n >= 1:
+                for t in range(PACK):
+                    turn_y(n - 1, t, Y_BANKS[t])
+                    store_y(n - 1, t, nc.scalar.copy)
+            if n == 1:
+                quantise_p2(5)
+            if n == 2:
+                quantise_p2(7)
+            x2q[n] = quantise(woven[:], "x2", 2)
+            if n < 2:
+                quantise_p2((4, 6)[n])
+            for s in range(PACK):
+                project2(n + 1, s, (2, 3))
+            for s in range(PACK):
+                project3(n, s, Y_BANKS[s])
+
+        for s in range(PACK):
+            subtract2(last, s, 0, PACK)
+        woven_early = weave_x2(nc.scalar.copy, last, 0, HALF)
+        woven_late = weave_x2(nc.scalar.copy, last, HALF, W)
+        for s in range(PACK - 1):
+            gate3(last - 1, s, acc3[last - 1, s], 0, W)
+        early = quantise(woven_early[:], "x2", 2)
+        project_half(acc_early, p3q, early, 0)
+        gate3(last - 1, PACK - 1, acc3[last - 1, PACK - 1], 0, W)
+        late = quantise(woven_late[:], "x2", 2)
+        for t in range(PACK):
+            if t == 2:
+                project_half(acc_late, p3q, late, 2)
+            turn_y(last - 1, t, Y_BANKS[t])
+            store_y(last - 1, t, nc.scalar.copy)
+        for s in range(PACK):
+            gate3(last, s, acc_early[s], 0, HALF)
+        turn_y(last, 0, MM_BANKS[0])
+        turn_y(last, 1, MM_BANKS[1])
+        for s in range(PACK):
+            gate3(last, s, acc_late[s], HALF, W)
+        turn_y(last, 2, MM_BANKS[2])
+        turn_y(last, 3, MM_BANKS[3])
+        for t in range(PACK):
+            store_y(last, t, nc.vector.tensor_copy if t % 2 else nc.scalar.copy)

@@ -21,6 +21,10 @@ W = 512
 HALF = W // 2
 GROUPS = M // W
 POOL_COLS = 784
+POOL_COLS_LAST = 544
+WARM_FIRST = 16
+WARM_NEXT = 8
+WARM_KEEP = 0
 
 
 def tile_gated_relaxed_block_projections_t1_kernel(tc, x, p1, p2, p3, g1, g2, g3, out):
@@ -146,12 +150,12 @@ def tile_gated_relaxed_block_projections_t1_kernel(tc, x, p1, p2, p3, g1, g2, g3
             acc1[g, s] = bank(MM_BANKS[s])[:]
             mx_pass(acc1[g, s], p1q, s, xq[g], 0, True, True)
 
-        def project_half(accs, weight, operand, first_bank):
+        def project_half(accs, weight, operand, banks, first_col=0):
             for pair in range(2):
-                bk = bank(MM_BANKS[first_bank + pair])
+                bk = bank(banks[pair])
                 for s in (2 * pair, 2 * pair + 1):
                     accs[s] = bk[:, HALF * (s % 2) : HALF * (s % 2 + 1)]
-                    mx_pass(accs[s], weight, s, operand, 0, True, True)
+                    mx_pass(accs[s], weight, s, operand, first_col, True, True)
 
         def gate1(g, s, acc, lo, hi):
             nc.vector.scalar_tensor_tensor(
@@ -165,7 +169,7 @@ def tile_gated_relaxed_block_projections_t1_kernel(tc, x, p1, p2, p3, g1, g2, g3
 
         def turn_x1(g, s, b):
             if s == 0:
-                x1b[g] = sbuf("x1b", 2, [P, PACK * W], BF16)
+                x1b[g] = sbuf("x1b" if g else "stage_shared", 2 if g else 1, [P, PACK * W], BF16)
             bk = bank(b)
             for t in range(PACK):
                 nc.tensor.transpose(bk[:, P * t : P * (t + 1)], run[g][:, s, P * t : P * (t + 1)], ident[:])
@@ -188,9 +192,9 @@ def tile_gated_relaxed_block_projections_t1_kernel(tc, x, p1, p2, p3, g1, g2, g3
             src = raw[n, 2 * kk + k][:, :, c0 : c0 + hi - lo]
             return stage[i][:, PACK * lo : PACK * hi], src
 
-        def weave_scalar(i, lo, hi):
+        def weave_scalar(i, lo, hi, copy=nc.scalar.copy):
             dst, src = stage_views(i, lo, hi)
-            nc.scalar.copy(out=dst.rearrange("p (c i j) -> p c j i", i=4, j=PACK), in_=src.rearrange("p j (c i) -> p c j i", i=4))
+            copy(out=dst.rearrange("p (c i j) -> p c j i", i=4, j=PACK), in_=src.rearrange("p j (c i) -> p c j i", i=4))
 
         def weave_pool(i, lo, hi):
             dst, src = stage_views(i, lo, hi)
@@ -203,25 +207,29 @@ def tile_gated_relaxed_block_projections_t1_kernel(tc, x, p1, p2, p3, g1, g2, g3
                 op1=ADD,
             )
 
-        def weave_shared(i):
-            stage[i] = sbuf("stage_shared", 1, [P, 2 * PACK * W], BF16)
+        def weave_shared(i, split):
+            stage[i] = sbuf("stage_shared" if i else "stage_first", 1, [P, 2 * PACK * W], BF16)
             weave_pool(i, 0, W)
-            weave_pool(i, W, POOL_COLS)
-            weave_scalar(i, POOL_COLS, 2 * W)
+            weave_pool(i, W, split)
+            if i > 1:
+                weave_scalar(i, split, 2 * W)
 
-        def weave_quarter(i, q):
+        def weave_quarter(i, q, copy=nc.scalar.copy):
             if q == 0:
                 stage[i] = sbuf("stage_scalar", 2, [P, 2 * PACK * W], BF16)
-            weave_scalar(i, 256 * q, 256 * (q + 1))
+            weave_scalar(i, 256 * q, 256 * (q + 1), copy)
 
         def quantise_p2(i):
-            p2q[i] = quantise(stage[i][:], "p2", 8)
+            n, kk = divmod(i, 2)
+            made = quantise(stage[i][:], "p2", 7)
+            p2q[n, 2 * kk] = (made, 0)
+            p2q[n, 2 * kk + 1] = (made, W)
 
         def project2(n, s, ks):
             for k in ks:
                 if k == 0:
                     acc2[n, s] = bank(MM_BANKS[s])
-                mx_pass(acc2[n, s][:], x1q[k], s, p2q[2 * n + k // 2], W * (k % 2), k == 0, k == GROUPS - 1)
+                mx_pass(acc2[n, s][:], x1q[k], s, p2q[n, k][0], p2q[n, k][1], k == 0, k == GROUPS - 1)
 
         def subtract2(n, s, t0, t1):
             rows = run[n][:, s, :].rearrange("q (t p) -> q t p", t=PACK)[:, t0:t1]
@@ -233,6 +241,18 @@ def tile_gated_relaxed_block_projections_t1_kernel(tc, x, p1, p2, p3, g1, g2, g3
             copy(
                 out=woven[:].rearrange("p (c i s) -> p c s i", i=4, s=PACK),
                 in_=run[n][:, :, lo:hi].rearrange("p s (c i) -> p c s i", i=4),
+            )
+            return woven
+
+        def weave_x2_pool(n, lo, hi):
+            woven = sbuf("wide", 4, [P, PACK * (hi - lo)], BF16)
+            nc.gpsimd.tensor_scalar(
+                out=woven[:].rearrange("p (c s) -> p c s", s=PACK),
+                in0=run[n][:, :, lo:hi].rearrange("p s c -> p c s"),
+                scalar1=1.0,
+                scalar2=0.0,
+                op0=MULT,
+                op1=ADD,
             )
             return woven
 
@@ -253,65 +273,85 @@ def tile_gated_relaxed_block_projections_t1_kernel(tc, x, p1, p2, p3, g1, g2, g3
                 nc.tensor.transpose(turned[n, t][:, P * s : P * (s + 1)], yt[n, s][:, P * t : P * (t + 1)], ident[:])
 
         def store_y(n, t, copy):
-            rows = sbuf("rows", 4, [P, W], F32)
+            rows = sbuf("raw", 14, [P, W], F32)
             copy(out=rows[:].rearrange("p (f s) -> p f s", s=PACK), in_=turned[n, t][:].rearrange("p (s f) -> p f s", s=PACK))
             nc.sync.dma_start(out=out_rows[n, t], in_=rows[:])
 
+        def warm_up(count, b):
+            bk = bank(b)
+            for i in range(count):
+                mx_pass(bk[:, :P], ones_q, 0, ones_q, 0, True, True)
+
+        ones = sbuf("ones", 1, [P, W], BF16)
+        nc.vector.memset(ones[:], 1.0)
+        ones_q = quantise(ones[:], "ones", 1)
+        warm_up(WARM_FIRST, 7)
         turn_x(0, 0, 0)
+        warm_up(WARM_NEXT, 7)
         p1g = sbuf("grouped", 1, [P, PACK * W], BF16)
         regroup_weight(nc.vector.tensor_copy, p1g, "p1", 0)
         regroup_weight(nc.vector.tensor_copy, p1g, "p1", 1)
         early = quantise(xt[0][:, : PACK * HALF], "x", 3)
         p1q = quantise(p1g[:], "p1", 1)
         turn_x(0, 1, 1)
-        acc_early = {}
-        acc_late = {}
-        project_half(acc_early, p1q, early, 0)
-        p3g = sbuf("stage_shared", 1, [P, PACK * W], BF16)
+        turn_x(1, 0, 0)
+        turn_x(1, 1, 5)
+        p3g = sbuf("stage_first", 1, [P, PACK * W], BF16)
         regroup_weight(nc.scalar.copy, p3g, "p3", 0)
         regroup_weight(nc.scalar.copy, p3g, "p3", 1)
-        turn_x(1, 0, 0)
+        acc_early = {}
+        acc_late = {}
+        project_half(acc_early, p1q, early, MM_BANKS[:2])
         late = quantise(xt[0][:, PACK * HALF :], "x", 3)
-        project_half(acc_late, p1q, late, 2)
-        turn_x(1, 1, 1)
+        project_half(acc_late, p1q, late, MM_BANKS[2:])
         for s in range(PACK):
             gate1(0, s, acc_early[s], 0, HALF)
+        xq[1] = quantise(xt[1][:], "x", 3)
+        project1(1, 0)
+        project1(1, 1)
         for s in range(PACK):
             gate1(0, s, acc_late[s], HALF, W)
-        xq[1] = quantise(xt[1][:], "x", 3)
         p3q = quantise(p3g[:], "p3", 1)
-        turn_x1(0, 0, 5)
-        turn_x1(0, 1, 0)
-        for s in range(PACK):
-            project1(1, s)
-        turn_x1(0, 2, 1)
-        turn_x1(0, 3, 5)
+        turn_x1(0, 0, 0)
+        turn_x1(0, 1, 1)
+        project1(1, 2)
+        project1(1, 3)
+        turn_x1(0, 2, 5)
+        turn_x1(0, 3, 0)
         spread_g2(0)
 
         for g in range(1, GROUPS):
-            weave_shared((0, 1, 3)[g - 1])
+            if g + 1 < GROUPS:
+                turn_x(g + 1, 0, 1)
+                turn_x(g + 1, 1, 5)
+            weave_shared((0, 1, 3)[g - 1], POOL_COLS)
             if g == 2:
                 load_p2(4)
             if g == 3:
                 load_p2(6)
-            if g + 1 < GROUPS:
-                turn_x(g + 1, 0, 0)
-                turn_x(g + 1, 1, 1)
             for s in range(PACK):
                 gate1(g, s, acc1[g, s], 0, W)
-                turn_x1(g, s, (5, 0, 1, 5)[s])
+                turn_x1(g, s, (5, 0, 1, 5)[s] if g == GROUPS - 1 else MM_BANKS[s])
+                if s == 1 and WARM_KEEP and g < GROUPS - 1:
+                    warm_up(WARM_KEEP, 0)
             gate2(g - 1)
             if g == GROUPS - 1:
                 for s in range(PACK):
                     project2(0, s, (0, 1, 2))
-            spread_g2(g)
             if g < GROUPS - 1:
-                weave_quarter(2, 2 * g - 2)
-                weave_quarter(2, 2 * g - 1)
+                if g == 1:
+                    weave_scalar(0, POOL_COLS, 2 * W)
+                    weave_quarter(2, 0)
+                else:
+                    weave_scalar(1, POOL_COLS, 2 * W)
+                    weave_quarter(2, 1)
+                    weave_quarter(2, 2)
                 xq[g + 1] = quantise(xt[g + 1][:], "x", 3)
                 for s in range(PACK):
                     project1(g + 1, s)
+                spread_g2(g)
             else:
+                weave_quarter(2, 3)
                 weave_quarter(5, 0)
                 weave_quarter(5, 1)
             if g < GROUPS - 1:
@@ -321,65 +361,89 @@ def tile_gated_relaxed_block_projections_t1_kernel(tc, x, p1, p2, p3, g1, g2, g3
             if g == GROUPS - 1:
                 for s in range(PACK):
                     project2(0, s, (3,))
+                spread_g2(g)
                 quantise_p2(2)
-            quantise_p2((0, 1, 3)[g - 1])
+            if g == 2:
+                quantise_p2(0)
+            if g > 1:
+                quantise_p2((1, 3)[g - 2])
 
         load_p2(7)
         last = GROUPS - 1
         for n in range(last):
-            weave_shared((4, 6, 7)[n])
-            for s in range(PACK):
-                subtract2(n, s, 0, PACK)
-            woven = weave_x2(nc.scalar.copy, n, 0, W)
-            project2(n + 1, 0, (0, 1))
-            project2(n + 1, 1, (0, 1))
+            if n < 2:
+                weave_shared((4, 6)[n], POOL_COLS)
+            else:
+                tail_stage = sbuf("stage_shared", 1, [P, 2 * PACK * W], BF16)
+                stage[7] = tail_stage
+                weave_pool(7, W, W + HALF)
+                weave_scalar(7, W + HALF, 2 * W)
             if n == 0:
                 weave_quarter(5, 2)
-                weave_quarter(5, 3)
+            for s in range(PACK):
+                subtract2(n, s, 0, PACK)
+                project2(n + 1, s, (0, 1, 2, 3) if n < 2 else (0, 1, 2))
+            woven = weave_x2(nc.scalar.copy, n, 0, W)
+            if n == 2:
+                p2q[last, 3] = (quantise(tail_stage[:, PACK * W :], "p2_tail", 2), 0)
+                for s in range(PACK):
+                    project2(last, s, (3,))
+            if n == 0:
+                weave_quarter(7, 0)
+                weave_quarter(7, 1)
                 gate2(last)
             else:
                 for s in range(PACK):
                     gate3(n - 1, s, acc3[n - 1, s], 0, W)
-            project2(n + 1, 2, (0, 1))
-            project2(n + 1, 3, (0, 1))
-            if n >= 1:
-                for t in range(PACK):
+                for t in range(PACK if n == 1 else 2):
                     turn_y(n - 1, t, Y_BANKS[t])
                     store_y(n - 1, t, nc.scalar.copy)
-            if n == 1:
-                quantise_p2(5)
-            if n == 2:
-                quantise_p2(7)
+            if n == 0:
+                weave_quarter(5, 3, nc.vector.tensor_copy)
             x2q[n] = quantise(woven[:], "x2", 2)
+            if n == 0:
+                quantise_p2(5)
+            if n == 1:
+                p2q[last, 2] = (quantise(stage[7][:, : PACK * W], "p2_tail", 2), 0)
             if n < 2:
                 quantise_p2((4, 6)[n])
-            for s in range(PACK):
-                project2(n + 1, s, (2, 3))
-            for s in range(PACK):
-                project3(n, s, Y_BANKS[s])
+                for s in range(PACK):
+                    project3(n, s, Y_BANKS[s])
 
+        project_half(acc_early, p3q, x2q[last - 1], Y_BANKS[2:])
+        for t in range(2, PACK):
+            turn_y(last - 2, t, Y_BANKS[t - 2])
+            store_y(last - 2, t, nc.scalar.copy)
         for s in range(PACK):
-            subtract2(last, s, 0, PACK)
-        woven_early = weave_x2(nc.scalar.copy, last, 0, HALF)
+            subtract2(last, s, 0, 2)
+        woven_early = weave_x2_pool(last, 0, HALF)
+        for s in range(PACK):
+            gate3(last - 1, s, acc_early[s], 0, HALF)
+        project_half(acc_late, p3q, x2q[last - 1], Y_BANKS[2:], HALF)
+        turn_y(last - 1, 0, Y_BANKS[0])
+        turn_y(last - 1, 1, Y_BANKS[1])
+        store_y(last - 1, 0, nc.scalar.copy)
+        for s in range(PACK):
+            subtract2(last, s, 2, PACK)
+        warm_up(WARM_NEXT, MM_BANKS[0])
         woven_late = weave_x2(nc.scalar.copy, last, HALF, W)
-        for s in range(PACK - 1):
-            gate3(last - 1, s, acc3[last - 1, s], 0, W)
-        early = quantise(woven_early[:], "x2", 2)
-        project_half(acc_early, p3q, early, 0)
-        gate3(last - 1, PACK - 1, acc3[last - 1, PACK - 1], 0, W)
-        late = quantise(woven_late[:], "x2", 2)
-        for t in range(PACK):
-            if t == 2:
-                project_half(acc_late, p3q, late, 2)
+        store_y(last - 1, 1, nc.scalar.copy)
+        for s in range(PACK):
+            gate3(last - 1, s, acc_late[s], HALF, W)
+        for t in range(2, PACK):
             turn_y(last - 1, t, Y_BANKS[t])
             store_y(last - 1, t, nc.scalar.copy)
+        early = quantise(woven_early[:], "x2", 2)
+        late = quantise(woven_late[:], "x2", 2)
+        project_half(acc_early, p3q, early, MM_BANKS[:2])
+        project_half(acc_late, p3q, late, MM_BANKS[2:])
         for s in range(PACK):
             gate3(last, s, acc_early[s], 0, HALF)
-        turn_y(last, 0, MM_BANKS[0])
-        turn_y(last, 1, MM_BANKS[1])
+        turn_y(last, 0, Y_BANKS[0])
+        turn_y(last, 1, Y_BANKS[1])
         for s in range(PACK):
             gate3(last, s, acc_late[s], HALF, W)
-        turn_y(last, 2, MM_BANKS[2])
-        turn_y(last, 3, MM_BANKS[3])
+        turn_y(last, 2, MM_BANKS[0])
+        turn_y(last, 3, MM_BANKS[1])
         for t in range(PACK):
-            store_y(last, t, nc.vector.tensor_copy if t % 2 else nc.scalar.copy)
+            store_y(last, t, nc.vector.tensor_copy if t == 3 else nc.scalar.copy)

@@ -24,7 +24,6 @@ POOL_COLS = 784
 POOL_COLS_LAST = 544
 WARM_FIRST = 16
 WARM_NEXT = 8
-WARM_KEEP = 0
 
 
 def tile_gated_relaxed_block_projections_t1_kernel(tc, x, p1, p2, p3, g1, g2, g3, out):
@@ -66,7 +65,7 @@ def tile_gated_relaxed_block_projections_t1_kernel(tc, x, p1, p2, p3, g1, g2, g3
         nc.scalar.dma_start(out=g1_sb[:], in_=g1.rearrange("(p s) -> p s", s=PACK))
 
         x_rows = x.rearrange("(g p t) d -> g p t d", p=P, t=PACK)
-        out_rows = out.rearrange("(g p t) d -> g t p d", p=P, t=PACK)
+        out_rows = out.rearrange("(g p t) d -> g p t d", p=P, t=PACK)
         x_raw = {}
         raw = {}
 
@@ -75,40 +74,36 @@ def tile_gated_relaxed_block_projections_t1_kernel(tc, x, p1, p2, p3, g1, g2, g3
             nc.sync.dma_start(out=half[:].rearrange("p (t d) -> p t d", t=2), in_=x_rows[g, :, 2 * h : 2 * h + 2, :])
             x_raw[g, h] = half
 
-        def load_rows(key, rows):
-            piece = sbuf("raw", 14, [P, PACK, rows.shape[1]], BF16)
+        def load_rows(key, rows, tag, bufs):
+            piece = sbuf(tag, bufs, [P, PACK, rows.shape[1]], BF16)
             nc.sync.dma_start(out=piece[:], in_=rows.rearrange("(p j) c -> p j c", j=PACK))
             raw[key] = piece
 
-        def load_p2(i):
-            n, kk = divmod(i, 2)
-            for k in (2 * kk, 2 * kk + 1):
-                load_rows((n, k), p2[W * k : W * (k + 1), W * n : W * (n + 1)])
+        def load_p2(pair, k):
+            load_rows((pair, k), p2[W * k : W * (k + 1), 2 * W * pair : 2 * W * (pair + 1)], "raw", 7)
 
         load_x(0, 0)
-        load_rows(("p1", 0), p1[:, :HALF])
-        load_rows(("p1", 1), p1[:, HALF:])
+        load_rows("p1", p1, "wide", 5)
         load_x(0, 1)
         load_x(1, 0)
         load_x(1, 1)
-        load_rows(("p3", 0), p3[:, :HALF])
-        load_rows(("p3", 1), p3[:, HALF:])
+        load_rows("p3", p3, "wide", 5)
         nc.sync.dma_start(out=g2_sb[:], in_=g2.rearrange("(g p t) -> p g t", p=P, t=PACK))
+        load_p2(0, 0)
         load_x(2, 0)
         load_x(2, 1)
-        load_p2(0)
+        load_p2(0, 1)
         load_x(3, 0)
         load_x(3, 1)
-        load_p2(2)
-        load_p2(1)
+        load_p2(0, 2)
+        load_p2(0, 3)
         nc.sync.dma_start(out=g3_sb[:], in_=g3.rearrange("(p s) -> p s", s=PACK))
-        load_p2(3)
-        load_p2(5)
+        for k in range(GROUPS - 1):
+            load_p2(1, k)
 
         ident = sbuf("ident", 1, [P, P], F32)
         make_identity(nc, ident[:])
-        g2_f32 = sbuf("g2_f32", 1, [P, GROUPS * PACK], F32)
-        nc.gpsimd.tensor_copy(out=g2_f32[:], in_=g2_sb[:].rearrange("p g t -> p (g t)"))
+        g2_words = g2_sb[:].rearrange("p g t -> p (g t)").bitcast(F32)
 
         xt = {}
         xq = {}
@@ -120,17 +115,20 @@ def tile_gated_relaxed_block_projections_t1_kernel(tc, x, p1, p2, p3, g1, g2, g3
         x2b = {}
         x2q = {}
         yt = {}
+        passes = {}
+        y_rows = {}
         acc1 = {}
         acc2 = {}
         acc3 = {}
         g2_bank = {}
         turned = {}
         MM_BANKS = (2, 3, 4, 6)
-        Y_BANKS = (5, 0, 1, 7)
+        LATE_BANKS = (1, 7, 4, 6)
+        Y_BANKS = (5, 0, 2, 3)
 
         def turn_x(g, h, b):
             if h == 0:
-                xt[g] = sbuf("wide", 4, [P, PACK * W], BF16)
+                xt[g] = sbuf("wide", 5, [P, PACK * W], BF16)
                 run[g] = sbuf("run", 4, [P, PACK, W], F32)
             words = x_raw[g, h][:].bitcast(F32)
             bk = bank(b)
@@ -143,8 +141,8 @@ def tile_gated_relaxed_block_projections_t1_kernel(tc, x, p1, p2, p3, g1, g2, g3
 
         def regroup_weight(copy, grouped, key, h):
             dst = grouped[:].rearrange("p (s a b j) -> p a s b j", s=PACK, b=2, j=PACK)
-            src = raw[key, h][:].rearrange("p j (a b s) -> p a s b j", s=PACK, b=2)
-            copy(out=dst[:, 32 * h : 32 * (h + 1)], in_=src)
+            src = raw[key][:].rearrange("p j (a b s) -> p a s b j", s=PACK, b=2)
+            copy(out=dst[:, 32 * h : 32 * (h + 1)], in_=src[:, 32 * h : 32 * (h + 1)])
 
         def project1(g, s):
             acc1[g, s] = bank(MM_BANKS[s])[:]
@@ -178,18 +176,21 @@ def tile_gated_relaxed_block_projections_t1_kernel(tc, x, p1, p2, p3, g1, g2, g3
 
         def spread_g2(g):
             g2_bank[g] = bank(7)
-            for t in range(PACK):
-                col = PACK * g + t
-                nc.tensor.transpose(g2_bank[g][:, P * t : P * (t + 1)], g2_f32[:, col : col + 1].to_broadcast([P, P]), ident[:])
+            for u in range(2):
+                col = 2 * g + u
+                nc.tensor.transpose(g2_bank[g][:, P * u : P * (u + 1)], g2_words[:, col : col + 1].to_broadcast([P, P]), ident[:])
 
         def gate2(g):
+            gate = g2_bank[g][:, :HALF].bitcast(BF16).rearrange("q (u p e) -> q u e p", u=2, e=2)
             for s in range(PACK):
-                nc.vector.tensor_tensor(out=run[g][:, s, :], in0=run[g][:, s, :], in1=g2_bank[g][:], op=MULT)
+                rows = run[g][:, s, :].rearrange("q (u e p) -> q u e p", u=2, e=2)
+                nc.vector.tensor_tensor(out=rows, in0=rows, in1=gate, op=MULT)
 
         def stage_views(i, lo, hi):
             n, kk = divmod(i, 2)
             k, c0 = divmod(lo, W)
-            src = raw[n, 2 * kk + k][:, :, c0 : c0 + hi - lo]
+            c0 = c0 + W * (n % 2)
+            src = raw[n // 2, 2 * kk + k][:, :, c0 : c0 + hi - lo]
             return stage[i][:, PACK * lo : PACK * hi], src
 
         def weave_scalar(i, lo, hi, copy=nc.scalar.copy):
@@ -211,7 +212,7 @@ def tile_gated_relaxed_block_projections_t1_kernel(tc, x, p1, p2, p3, g1, g2, g3
             stage[i] = sbuf("stage_shared" if i else "stage_first", 1, [P, 2 * PACK * W], BF16)
             weave_pool(i, 0, W)
             weave_pool(i, W, split)
-            if i > 1:
+            if i > 2:
                 weave_scalar(i, split, 2 * W)
 
         def weave_quarter(i, q, copy=nc.scalar.copy):
@@ -227,28 +228,30 @@ def tile_gated_relaxed_block_projections_t1_kernel(tc, x, p1, p2, p3, g1, g2, g3
 
         def project2(n, s, ks):
             for k in ks:
-                if k == 0:
-                    acc2[n, s] = bank(MM_BANKS[s])
-                mx_pass(acc2[n, s][:], x1q[k], s, p2q[n, k][0], p2q[n, k][1], k == 0, k == GROUPS - 1)
+                start = (n, s) not in passes
+                if start:
+                    acc2[n, s] = bank((MM_BANKS if n < 2 else LATE_BANKS)[s])
+                passes[n, s] = passes.get((n, s), 0) + 1
+                mx_pass(acc2[n, s][:], x1q[k], s, p2q[n, k][0], p2q[n, k][1], start, passes[n, s] == GROUPS)
 
-        def subtract2(n, s, t0, t1):
+        def subtract2(n, s, t0, t1, into):
             rows = run[n][:, s, :].rearrange("q (t p) -> q t p", t=PACK)[:, t0:t1]
             acc = acc2[n, s][:].rearrange("q (p t) -> q t p", t=PACK)[:, t0:t1]
-            nc.vector.tensor_tensor(out=rows, in0=rows, in1=acc, op=SUBTRACT)
+            nc.vector.tensor_tensor(out=into[:, s, :].rearrange("q (t p) -> q t p", p=P), in0=rows, in1=acc, op=SUBTRACT)
 
-        def weave_x2(copy, n, lo, hi):
-            woven = sbuf("wide", 4, [P, PACK * (hi - lo)], BF16)
+        def weave_x2(copy, x2):
+            woven = sbuf("wide", 5, [P, PACK * x2.shape[2]], BF16)
             copy(
                 out=woven[:].rearrange("p (c i s) -> p c s i", i=4, s=PACK),
-                in_=run[n][:, :, lo:hi].rearrange("p s (c i) -> p c s i", i=4),
+                in_=x2[:].rearrange("p s (c i) -> p c s i", i=4),
             )
             return woven
 
-        def weave_x2_pool(n, lo, hi):
-            woven = sbuf("wide", 4, [P, PACK * (hi - lo)], BF16)
+        def weave_x2_pool(x2):
+            woven = sbuf("wide", 5, [P, PACK * x2.shape[2]], BF16)
             nc.gpsimd.tensor_scalar(
                 out=woven[:].rearrange("p (c s) -> p c s", s=PACK),
-                in0=run[n][:, :, lo:hi].rearrange("p s c -> p c s"),
+                in0=x2[:].rearrange("p s c -> p c s"),
                 scalar1=1.0,
                 scalar2=0.0,
                 op0=MULT,
@@ -260,11 +263,11 @@ def tile_gated_relaxed_block_projections_t1_kernel(tc, x, p1, p2, p3, g1, g2, g3
             acc3[n, s] = bank(b)[:]
             mx_pass(acc3[n, s], p3q, s, x2q[n], 0, True, True)
 
-        def gate3(n, s, acc, lo, hi):
+        def gate3(n, s, x2, acc, lo, hi):
             if lo == 0:
                 yt[n, s] = sbuf("half", 8, [P, W], F32)
             nc.vector.scalar_tensor_tensor(
-                out=yt[n, s][:, lo:hi], in0=run[n][:, s, lo:hi], scalar=g3_sb[:, s : s + 1], in1=acc, op0=MULT, op1=SUBTRACT
+                out=yt[n, s][:, lo:hi], in0=x2, scalar=g3_sb[:, s : s + 1], in1=acc, op0=MULT, op1=SUBTRACT
             )
 
         def turn_y(n, t, b):
@@ -273,9 +276,14 @@ def tile_gated_relaxed_block_projections_t1_kernel(tc, x, p1, p2, p3, g1, g2, g3
                 nc.tensor.transpose(turned[n, t][:, P * s : P * (s + 1)], yt[n, s][:, P * t : P * (t + 1)], ident[:])
 
         def store_y(n, t, copy):
-            rows = sbuf("raw", 14, [P, W], F32)
-            copy(out=rows[:].rearrange("p (f s) -> p f s", s=PACK), in_=turned[n, t][:].rearrange("p (s f) -> p f s", s=PACK))
-            nc.sync.dma_start(out=out_rows[n, t], in_=rows[:])
+            if t % 2 == 0:
+                y_rows[n, t // 2] = sbuf("raw", 7, [P, 2, W], F32)
+            rows = y_rows[n, t // 2]
+            copy(out=rows[:, t % 2, :].rearrange("p (f s) -> p f s", s=PACK), in_=turned[n, t][:].rearrange("p (s f) -> p f s", s=PACK))
+            if n == GROUPS - 1:
+                nc.sync.dma_start(out=out_rows[n, :, t, :], in_=rows[:, t % 2, :])
+            elif t % 2:
+                nc.sync.dma_start(out=out_rows[n, :, t - 1 : t + 1, :], in_=rows[:])
 
         def warm_up(count, b):
             bk = bank(b)
@@ -288,7 +296,7 @@ def tile_gated_relaxed_block_projections_t1_kernel(tc, x, p1, p2, p3, g1, g2, g3
         warm_up(WARM_FIRST, 7)
         turn_x(0, 0, 0)
         warm_up(WARM_NEXT, 7)
-        p1g = sbuf("grouped", 1, [P, PACK * W], BF16)
+        p1g = sbuf("x1b", 2, [P, PACK * W], BF16)
         regroup_weight(nc.vector.tensor_copy, p1g, "p1", 0)
         regroup_weight(nc.vector.tensor_copy, p1g, "p1", 1)
         early = quantise(xt[0][:, : PACK * HALF], "x", 3)
@@ -321,54 +329,55 @@ def tile_gated_relaxed_block_projections_t1_kernel(tc, x, p1, p2, p3, g1, g2, g3
         spread_g2(0)
 
         for g in range(1, GROUPS):
+            weave_shared((0, 2, 3)[g - 1], POOL_COLS)
+            if g == 2:
+                weave_scalar(2, POOL_COLS, 2 * W)
             if g + 1 < GROUPS:
                 turn_x(g + 1, 0, 1)
                 turn_x(g + 1, 1, 5)
-            weave_shared((0, 1, 3)[g - 1], POOL_COLS)
             if g == 2:
-                load_p2(4)
-            if g == 3:
-                load_p2(6)
+                turn_x1(1, 2, 0)
+                turn_x1(1, 3, 1)
             for s in range(PACK):
                 gate1(g, s, acc1[g, s], 0, W)
-                turn_x1(g, s, (5, 0, 1, 5)[s] if g == GROUPS - 1 else MM_BANKS[s])
-                if s == 1 and WARM_KEEP and g < GROUPS - 1:
-                    warm_up(WARM_KEEP, 0)
+                if g == 1:
+                    if s < 2:
+                        turn_x1(g, s, s)
+                else:
+                    turn_x1(g, s, (5, 0, 1, 5)[s] if g == GROUPS - 1 else MM_BANKS[s])
             gate2(g - 1)
             if g == GROUPS - 1:
                 for s in range(PACK):
-                    project2(0, s, (0, 1, 2))
+                    project2(0, s, (0, 1))
             if g < GROUPS - 1:
                 if g == 1:
                     weave_scalar(0, POOL_COLS, 2 * W)
-                    weave_quarter(2, 0)
                 else:
-                    weave_scalar(1, POOL_COLS, 2 * W)
-                    weave_quarter(2, 1)
-                    weave_quarter(2, 2)
+                    load_p2(1, GROUPS - 1)
+                    for q in range(3):
+                        weave_quarter(1, q)
                 xq[g + 1] = quantise(xt[g + 1][:], "x", 3)
                 for s in range(PACK):
                     project1(g + 1, s)
                 spread_g2(g)
             else:
-                weave_quarter(2, 3)
+                weave_quarter(1, 3, nc.vector.tensor_copy)
                 weave_quarter(5, 0)
                 weave_quarter(5, 1)
             if g < GROUPS - 1:
                 x1q[g - 1] = quantise(x1b[g - 1][:], "x1", 4)
-            if g > 1:
-                x1q[g] = quantise(x1b[g][:], "x1", 4)
-            if g == GROUPS - 1:
-                for s in range(PACK):
-                    project2(0, s, (3,))
-                spread_g2(g)
-                quantise_p2(2)
             if g == 2:
                 quantise_p2(0)
             if g > 1:
-                quantise_p2((1, 3)[g - 2])
+                x1q[g] = quantise(x1b[g][:], "x1", 4)
+            if g == GROUPS - 1:
+                quantise_p2(1)
+                spread_g2(g)
+                for s in range(PACK):
+                    project2(0, s, (3, 2))
+            if g > 1:
+                quantise_p2(g)
 
-        load_p2(7)
         last = GROUPS - 1
         for n in range(last):
             if n < 2:
@@ -381,9 +390,12 @@ def tile_gated_relaxed_block_projections_t1_kernel(tc, x, p1, p2, p3, g1, g2, g3
             if n == 0:
                 weave_quarter(5, 2)
             for s in range(PACK):
-                subtract2(n, s, 0, PACK)
-                project2(n + 1, s, (0, 1, 2, 3) if n < 2 else (0, 1, 2))
-            woven = weave_x2(nc.scalar.copy, n, 0, W)
+                subtract2(n, s, 0, PACK, run[n])
+                if n == 1 and s < 2:
+                    project3(0, s + 2, Y_BANKS[s + 2])
+                else:
+                    project2(n + 1, s, (0, 1, 2, 3) if n < 2 else (0, 1, 2))
+            woven = weave_x2(nc.scalar.copy, run[n])
             if n == 2:
                 p2q[last, 3] = (quantise(tail_stage[:, PACK * W :], "p2_tail", 2), 0)
                 for s in range(PACK):
@@ -394,7 +406,7 @@ def tile_gated_relaxed_block_projections_t1_kernel(tc, x, p1, p2, p3, g1, g2, g3
                 gate2(last)
             else:
                 for s in range(PACK):
-                    gate3(n - 1, s, acc3[n - 1, s], 0, W)
+                    gate3(n - 1, s, run[n - 1][:, s, :], acc3[n - 1, s], 0, W)
                 for t in range(PACK if n == 1 else 2):
                     turn_y(n - 1, t, Y_BANKS[t])
                     store_y(n - 1, t, nc.scalar.copy)
@@ -407,43 +419,49 @@ def tile_gated_relaxed_block_projections_t1_kernel(tc, x, p1, p2, p3, g1, g2, g3
                 p2q[last, 2] = (quantise(stage[7][:, : PACK * W], "p2_tail", 2), 0)
             if n < 2:
                 quantise_p2((4, 6)[n])
-                for s in range(PACK):
+                for s in range(PACK if n else 2):
                     project3(n, s, Y_BANKS[s])
+            if n == 0:
+                project2(2, 0, (2, 3))
+                project2(2, 1, (2, 3, 0, 1))
+                project2(2, 0, (0, 1))
 
         project_half(acc_early, p3q, x2q[last - 1], Y_BANKS[2:])
         for t in range(2, PACK):
-            turn_y(last - 2, t, Y_BANKS[t - 2])
+            turn_y(last - 2, t, Y_BANKS[t % 2])
             store_y(last - 2, t, nc.scalar.copy)
+        x2_early = sbuf("wide", 5, [P, PACK, HALF], F32)
+        x2_late = sbuf("wide", 5, [P, PACK, HALF], F32)
         for s in range(PACK):
-            subtract2(last, s, 0, 2)
-        woven_early = weave_x2_pool(last, 0, HALF)
+            subtract2(last, s, 0, 2, x2_early)
+        woven_early = weave_x2_pool(x2_early)
         for s in range(PACK):
-            gate3(last - 1, s, acc_early[s], 0, HALF)
+            gate3(last - 1, s, run[last - 1][:, s, :HALF], acc_early[s], 0, HALF)
         project_half(acc_late, p3q, x2q[last - 1], Y_BANKS[2:], HALF)
         turn_y(last - 1, 0, Y_BANKS[0])
         turn_y(last - 1, 1, Y_BANKS[1])
         store_y(last - 1, 0, nc.scalar.copy)
         for s in range(PACK):
-            subtract2(last, s, 2, PACK)
-        warm_up(WARM_NEXT, MM_BANKS[0])
-        woven_late = weave_x2(nc.scalar.copy, last, HALF, W)
+            subtract2(last, s, 2, PACK, x2_late)
+        warm_up(WARM_NEXT, LATE_BANKS[0])
+        woven_late = weave_x2(nc.scalar.copy, x2_late)
         store_y(last - 1, 1, nc.scalar.copy)
         for s in range(PACK):
-            gate3(last - 1, s, acc_late[s], HALF, W)
+            gate3(last - 1, s, run[last - 1][:, s, HALF:], acc_late[s], HALF, W)
         for t in range(2, PACK):
             turn_y(last - 1, t, Y_BANKS[t])
             store_y(last - 1, t, nc.scalar.copy)
         early = quantise(woven_early[:], "x2", 2)
         late = quantise(woven_late[:], "x2", 2)
-        project_half(acc_early, p3q, early, MM_BANKS[:2])
-        project_half(acc_late, p3q, late, MM_BANKS[2:])
+        project_half(acc_early, p3q, early, LATE_BANKS[:2])
+        project_half(acc_late, p3q, late, LATE_BANKS[2:])
         for s in range(PACK):
-            gate3(last, s, acc_early[s], 0, HALF)
+            gate3(last, s, x2_early[:, s, :], acc_early[s], 0, HALF)
         turn_y(last, 0, Y_BANKS[0])
         turn_y(last, 1, Y_BANKS[1])
         for s in range(PACK):
-            gate3(last, s, acc_late[s], HALF, W)
-        turn_y(last, 2, MM_BANKS[0])
-        turn_y(last, 3, MM_BANKS[1])
+            gate3(last, s, x2_late[:, s, :], acc_late[s], HALF, W)
+        turn_y(last, 2, LATE_BANKS[0])
+        turn_y(last, 3, LATE_BANKS[1])
         for t in range(PACK):
-            store_y(last, t, nc.vector.tensor_copy if t == 3 else nc.scalar.copy)
+            store_y(last, t, nc.vector.tensor_copy if t == 2 else nc.scalar.copy)

@@ -20,10 +20,32 @@ PACK = 4
 W = 512
 HALF = W // 2
 GROUPS = M // W
-POOL_COLS = 784
-POOL_COLS_LAST = 544
-WARM_FIRST = 16
-WARM_NEXT = 8
+LAST = GROUPS - 1
+
+BATCHES = (
+    ((0, 0), (1, 0)),
+    ((0, 2), (0, 3)),
+    ((0, 1), (1, 1)),
+    ((1, 2), (1, 3)),
+    ((2, 0), (2, 1)),
+    ((2, 2), (2, 3)),
+    ((3, 0), (3, 1)),
+    ((3, 2), (3, 3)),
+)
+GPSIMD_COLS = 768
+QUARTER = 2 * W // 4
+WARM_AT_START = 16
+WARM_IN_GAP = 8
+
+EARLY_BANKS = (2, 3, 4, 6)
+LATE_BANKS = (1, 7, 4, 6)
+Y_BANKS = (5, 0, 2, 3)
+TURN_BANKS = (0, 1, 5)
+G2_BANK = 7
+
+HALF_BUFS = 8
+WIDE_BUFS = 5
+RAW_BUFS = 7
 
 
 def tile_gated_relaxed_block_projections_t1_kernel(tc, x, p1, p2, p3, g1, g2, g3, out):
@@ -39,22 +61,22 @@ def tile_gated_relaxed_block_projections_t1_kernel(tc, x, p1, p2, p3, g1, g2, g3
         def bank(b):
             return ps.tile([P, W], F32, name="bank%d" % b, tag="bank%d" % b)
 
-        def quantise(src, tag, bufs):
-            words = src.shape[1] // PACK
+        def quantise(woven, tag, bufs):
+            words = woven.shape[1] // PACK
             codes = sbuf(tag + "_codes", bufs, [P, words], U32)
             scales = sbuf(tag + "_scales", bufs, [P, words], U8)
-            nc.vector.quantize_mx(out=codes[:].bitcast(FP8X4), scales=scales[:], in_=src)
+            nc.vector.quantize_mx(out=codes[:].bitcast(FP8X4), scales=scales[:], in_=woven)
             return codes, scales
 
-        def mx_pass(acc, stat, s, mov, first_col, start, stop):
+        def mx_pass(acc, stationary, s, moving, first_col, start, stop):
             cols = slice(P * s, P * (s + 1))
             span = slice(first_col, first_col + acc.shape[1])
             nc.tensor.matmul_mx(
                 out=acc,
-                lhsT=stat[0][:, cols].bitcast(FP8X4),
-                lhsT_scale=stat[1][:, cols],
-                rhs=mov[0][:, span].bitcast(FP8X4),
-                rhs_scale=mov[1][:, span],
+                lhsT=stationary[0][:, cols].bitcast(FP8X4),
+                lhsT_scale=stationary[1][:, cols],
+                rhs=moving[0][:, span].bitcast(FP8X4),
+                rhs_scale=moving[1][:, span],
                 start=start,
                 stop=stop,
             )
@@ -64,141 +86,143 @@ def tile_gated_relaxed_block_projections_t1_kernel(tc, x, p1, p2, p3, g1, g2, g3
         g2_sb = sbuf("g2", 1, [P, GROUPS, PACK], BF16)
         nc.scalar.dma_start(out=g1_sb[:], in_=g1.rearrange("(p s) -> p s", s=PACK))
 
-        x_rows = x.rearrange("(g p t) d -> g p t d", p=P, t=PACK)
-        out_rows = out.rearrange("(g p t) d -> g p t d", p=P, t=PACK)
+        x_rows = x.rearrange("(g r t) d -> g r t d", r=P, t=PACK)
+        out_rows = out.rearrange("(g r t) d -> g r t d", r=P, t=PACK)
         x_raw = {}
         raw = {}
 
         def load_x(g, h):
-            half = sbuf("half", 8, [P, 2 * D], BF16)
-            nc.sync.dma_start(out=half[:].rearrange("p (t d) -> p t d", t=2), in_=x_rows[g, :, 2 * h : 2 * h + 2, :])
-            x_raw[g, h] = half
+            x_raw[g, h] = sbuf("half", HALF_BUFS, [P, 2 * D], BF16)
+            nc.sync.dma_start(out=x_raw[g, h][:].rearrange("r (t d) -> r t d", t=2), in_=x_rows[g, :, 2 * h : 2 * h + 2, :])
 
         def load_rows(key, rows, tag, bufs):
-            piece = sbuf(tag, bufs, [P, PACK, rows.shape[1]], BF16)
-            nc.sync.dma_start(out=piece[:], in_=rows.rearrange("(p j) c -> p j c", j=PACK))
-            raw[key] = piece
+            raw[key] = sbuf(tag, bufs, [P, PACK, rows.shape[1]], BF16)
+            nc.sync.dma_start(out=raw[key][:], in_=rows.rearrange("(p j) c -> p j c", j=PACK))
 
         def load_p2(pair, k):
-            load_rows((pair, k), p2[W * k : W * (k + 1), 2 * W * pair : 2 * W * (pair + 1)], "raw", 7)
+            load_rows((pair, k), p2[W * k : W * (k + 1), 2 * W * pair : 2 * W * (pair + 1)], "raw", RAW_BUFS)
 
         load_x(0, 0)
-        load_rows("p1", p1, "wide", 5)
+        load_rows("p1", p1, "wide", WIDE_BUFS)
         load_x(0, 1)
         load_x(1, 0)
         load_x(1, 1)
-        load_rows("p3", p3, "wide", 5)
-        nc.sync.dma_start(out=g2_sb[:], in_=g2.rearrange("(g p t) -> p g t", p=P, t=PACK))
+        load_rows("p3", p3, "wide", WIDE_BUFS)
+        nc.sync.dma_start(out=g2_sb[:], in_=g2.rearrange("(g r t) -> r g t", r=P, t=PACK))
         load_p2(0, 0)
         load_x(2, 0)
         load_x(2, 1)
         load_p2(0, 1)
+        load_p2(0, 2)
         load_x(3, 0)
         load_x(3, 1)
-        load_p2(0, 2)
         load_p2(0, 3)
         nc.sync.dma_start(out=g3_sb[:], in_=g3.rearrange("(p s) -> p s", s=PACK))
-        for k in range(GROUPS - 1):
-            load_p2(1, k)
+        load_p2(1, 2)
+        load_p2(1, 3)
+        load_p2(1, 0)
 
         ident = sbuf("ident", 1, [P, P], F32)
         make_identity(nc, ident[:])
-        g2_words = g2_sb[:].rearrange("p g t -> p (g t)").bitcast(F32)
 
-        xt = {}
-        xq = {}
-        run = {}
-        x1b = {}
-        x1q = {}
-        stage = {}
-        p2q = {}
-        x2b = {}
-        x2q = {}
-        yt = {}
-        passes = {}
+        x_woven = {}
+        x_mx = {}
+        running = {}
+        x1_woven = {}
+        x1_mx = {}
+        p2_woven = {}
+        p2_mx = {}
+        x2_mx = {}
+        c1 = {}
+        c2 = {}
+        c2_passes = {}
+        c3 = {}
+        g2_spread = {}
+        y_turned = {}
+        y_bank = {}
         y_rows = {}
-        acc1 = {}
-        acc2 = {}
-        acc3 = {}
-        g2_bank = {}
-        turned = {}
-        MM_BANKS = (2, 3, 4, 6)
-        LATE_BANKS = (1, 7, 4, 6)
-        Y_BANKS = (5, 0, 2, 3)
 
         def turn_x(g, h, b):
             if h == 0:
-                xt[g] = sbuf("wide", 5, [P, PACK * W], BF16)
-                run[g] = sbuf("run", 4, [P, PACK, W], F32)
+                x_woven[g] = sbuf("wide", WIDE_BUFS, [P, PACK * W], BF16)
+                running[g] = sbuf("running", GROUPS, [P, PACK, W], F32)
             words = x_raw[g, h][:].bitcast(F32)
-            bk = bank(b)
+            turned = bank(b)
             for t in range(2):
                 for u in range(2):
-                    first = 256 * t + u
-                    nc.tensor.transpose(bk[:, P * (2 * t + u) : P * (2 * t + u + 1)], words[:, first : 256 * (t + 1) : 2], ident[:])
-            dst = xt[g][:].bitcast(F32)[:, W * h : W * (h + 1)]
-            nc.scalar.copy(out=dst.rearrange("p (t r u) -> p t r u", t=2, u=2), in_=bk[:].rearrange("p (t u r) -> p t r u", t=2, u=2))
+                    row = slice(HALF * t + u, HALF * (t + 1), 2)
+                    nc.tensor.transpose(turned[:, P * (2 * t + u) : P * (2 * t + u + 1)], words[:, row], ident[:])
+            dst = x_woven[g][:].bitcast(F32)[:, W * h : W * (h + 1)]
+            nc.scalar.copy(
+                out=dst.rearrange("p (t r u) -> p t r u", t=2, u=2),
+                in_=turned[:].rearrange("p (t u r) -> p t r u", t=2, u=2),
+            )
 
-        def regroup_weight(copy, grouped, key, h):
-            dst = grouped[:].rearrange("p (s a b j) -> p a s b j", s=PACK, b=2, j=PACK)
+        def weave_weight(copy, woven, key, h):
+            half = slice(P // 4 * h, P // 4 * (h + 1))
+            dst = woven[:].rearrange("p (s a b j) -> p a s b j", s=PACK, b=2, j=PACK)
             src = raw[key][:].rearrange("p j (a b s) -> p a s b j", s=PACK, b=2)
-            copy(out=dst[:, 32 * h : 32 * (h + 1)], in_=src[:, 32 * h : 32 * (h + 1)])
+            copy(out=dst[:, half], in_=src[:, half])
+
+        def quantise_x(g):
+            x_mx[g] = quantise(x_woven[g][:], "x", 3)
 
         def project1(g, s):
-            acc1[g, s] = bank(MM_BANKS[s])[:]
-            mx_pass(acc1[g, s], p1q, s, xq[g], 0, True, True)
+            c1[g, s] = bank(EARLY_BANKS[s])[:]
+            mx_pass(c1[g, s], p1_mx, s, x_mx[g], 0, True, True)
 
-        def project_half(accs, weight, operand, banks, first_col=0):
-            for pair in range(2):
-                bk = bank(banks[pair])
-                for s in (2 * pair, 2 * pair + 1):
-                    accs[s] = bk[:, HALF * (s % 2) : HALF * (s % 2 + 1)]
-                    mx_pass(accs[s], weight, s, operand, first_col, True, True)
+        def project_half(weight_mx, moving, first_col, banks):
+            sums = []
+            for b in banks:
+                both = bank(b)
+                for side in range(2):
+                    sums.append(both[:, HALF * side : HALF * (side + 1)])
+                    mx_pass(sums[-1], weight_mx, len(sums) - 1, moving, first_col, True, True)
+            return sums
 
-        def gate1(g, s, acc, lo, hi):
+        def gate1(g, s, product, lo, hi):
             nc.vector.scalar_tensor_tensor(
-                out=run[g][:, s, lo:hi],
-                in0=xt[g][:].rearrange("p (n j) -> p n j", j=PACK)[:, lo:hi, s],
+                out=running[g][:, s, lo:hi],
+                in0=x_woven[g][:].rearrange("p (n s) -> p n s", s=PACK)[:, lo:hi, s],
                 scalar=g1_sb[:, s : s + 1],
-                in1=acc,
+                in1=product,
                 op0=MULT,
                 op1=SUBTRACT,
             )
 
         def turn_x1(g, s, b):
-            if s == 0:
-                x1b[g] = sbuf("x1b" if g else "stage_shared", 2 if g else 1, [P, PACK * W], BF16)
-            bk = bank(b)
+            if s == 0 and g == 0:
+                x1_woven[g] = sbuf("gpsimd_batch", 1, [P, PACK * W], BF16)
+            elif s == 0:
+                x1_woven[g] = sbuf("x1_woven", 2, [P, PACK * W], BF16)
+            turned = bank(b)
             for t in range(PACK):
-                nc.tensor.transpose(bk[:, P * t : P * (t + 1)], run[g][:, s, P * t : P * (t + 1)], ident[:])
-            dst = x1b[g][:, W * s : W * (s + 1)]
-            nc.scalar.copy(out=dst.rearrange("p (f t) -> p f t", t=PACK), in_=bk[:].rearrange("p (t f) -> p f t", t=PACK))
+                nc.tensor.transpose(turned[:, P * t : P * (t + 1)], running[g][:, s, P * t : P * (t + 1)], ident[:])
+            nc.scalar.copy(
+                out=x1_woven[g][:, W * s : W * (s + 1)].rearrange("r (p t) -> r p t", t=PACK),
+                in_=turned[:].rearrange("r (t p) -> r p t", t=PACK),
+            )
+
+        def quantise_x1(g):
+            x1_mx[g] = quantise(x1_woven[g][:], "x1", GROUPS)
 
         def spread_g2(g):
-            g2_bank[g] = bank(7)
+            words = g2_sb[:].rearrange("r g t -> r (g t)").bitcast(F32)
+            g2_spread[g] = bank(G2_BANK)
             for u in range(2):
-                col = 2 * g + u
-                nc.tensor.transpose(g2_bank[g][:, P * u : P * (u + 1)], g2_words[:, col : col + 1].to_broadcast([P, P]), ident[:])
+                word = words[:, 2 * g + u : 2 * g + u + 1].to_broadcast([P, P])
+                nc.tensor.transpose(g2_spread[g][:, P * u : P * (u + 1)], word, ident[:])
 
         def gate2(g):
-            gate = g2_bank[g][:, :HALF].bitcast(BF16).rearrange("q (u p e) -> q u e p", u=2, e=2)
+            gates = g2_spread[g][:, :HALF].bitcast(BF16).rearrange("p (u r e) -> p u e r", u=2, e=2)
             for s in range(PACK):
-                rows = run[g][:, s, :].rearrange("q (u e p) -> q u e p", u=2, e=2)
-                nc.vector.tensor_tensor(out=rows, in0=rows, in1=gate, op=MULT)
+                rows = running[g][:, s, :].rearrange("p (u e r) -> p u e r", u=2, e=2)
+                nc.vector.tensor_tensor(out=rows, in0=rows, in1=gates, op=MULT)
 
-        def stage_views(i, lo, hi):
-            n, kk = divmod(i, 2)
-            k, c0 = divmod(lo, W)
-            c0 = c0 + W * (n % 2)
-            src = raw[n // 2, 2 * kk + k][:, :, c0 : c0 + hi - lo]
-            return stage[i][:, PACK * lo : PACK * hi], src
-
-        def weave_scalar(i, lo, hi, copy=nc.scalar.copy):
-            dst, src = stage_views(i, lo, hi)
+        def weave_by_copy(copy, dst, src):
             copy(out=dst.rearrange("p (c i j) -> p c j i", i=4, j=PACK), in_=src.rearrange("p j (c i) -> p c j i", i=4))
 
-        def weave_pool(i, lo, hi):
-            dst, src = stage_views(i, lo, hi)
+        def weave_on_gpsimd(dst, src):
             nc.gpsimd.tensor_scalar(
                 out=dst.rearrange("p (c j) -> p c j", j=PACK),
                 in0=src.rearrange("p j c -> p c j"),
@@ -208,260 +232,280 @@ def tile_gated_relaxed_block_projections_t1_kernel(tc, x, p1, p2, p3, g1, g2, g3
                 op1=ADD,
             )
 
-        def weave_shared(i, split):
-            stage[i] = sbuf("stage_shared" if i else "stage_first", 1, [P, 2 * PACK * W], BF16)
-            weave_pool(i, 0, W)
-            weave_pool(i, W, split)
-            if i > 2:
-                weave_scalar(i, split, 2 * W)
+        def batch_views(i, lo, hi):
+            n, k = BATCHES[i][lo // W]
+            first = W * (n % 2) + lo % W
+            return p2_woven[i][:, PACK * lo : PACK * hi], raw[n // 2, k][:, :, first : first + hi - lo]
 
-        def weave_quarter(i, q, copy=nc.scalar.copy):
+        def weave_gpsimd_share(i, tag):
+            p2_woven[i] = sbuf(tag, 1, [P, 2 * PACK * W], BF16)
+            weave_on_gpsimd(*batch_views(i, 0, W))
+            weave_on_gpsimd(*batch_views(i, W, GPSIMD_COLS))
+
+        def weave_scalar_share(i):
+            weave_by_copy(nc.scalar.copy, *batch_views(i, GPSIMD_COLS, 2 * W))
+
+        def weave_quarter(i, q, copy):
             if q == 0:
-                stage[i] = sbuf("stage_scalar", 2, [P, 2 * PACK * W], BF16)
-            weave_scalar(i, 256 * q, 256 * (q + 1), copy)
+                p2_woven[i] = sbuf("scalar_batch", 2, [P, 2 * PACK * W], BF16)
+            weave_by_copy(copy, *batch_views(i, QUARTER * q, QUARTER * (q + 1)))
 
-        def quantise_p2(i):
-            n, kk = divmod(i, 2)
-            made = quantise(stage[i][:], "p2", 7)
-            p2q[n, 2 * kk] = (made, 0)
-            p2q[n, 2 * kk + 1] = (made, W)
+        def quantise_batch(i):
+            made = quantise(p2_woven[i][:], "p2", len(BATCHES) - 1)
+            p2_mx[BATCHES[i][0]] = (made, 0)
+            p2_mx[BATCHES[i][1]] = (made, W)
+
+        def quantise_chunk(i, which):
+            woven = p2_woven[i][:, PACK * W * which : PACK * W * (which + 1)]
+            p2_mx[BATCHES[i][which]] = (quantise(woven, "p2_last", 2), 0)
 
         def project2(n, s, ks):
             for k in ks:
-                start = (n, s) not in passes
-                if start:
-                    acc2[n, s] = bank((MM_BANKS if n < 2 else LATE_BANKS)[s])
-                passes[n, s] = passes.get((n, s), 0) + 1
-                mx_pass(acc2[n, s][:], x1q[k], s, p2q[n, k][0], p2q[n, k][1], start, passes[n, s] == GROUPS)
+                done = c2_passes.get((n, s), 0)
+                if done == 0:
+                    c2[n, s] = bank((EARLY_BANKS if n < 2 else LATE_BANKS)[s])
+                c2_passes[n, s] = done + 1
+                mx_pass(c2[n, s][:], x1_mx[k], s, p2_mx[n, k][0], p2_mx[n, k][1], done == 0, done == LAST)
 
-        def subtract2(n, s, t0, t1, into):
-            rows = run[n][:, s, :].rearrange("q (t p) -> q t p", t=PACK)[:, t0:t1]
-            acc = acc2[n, s][:].rearrange("q (p t) -> q t p", t=PACK)[:, t0:t1]
-            nc.vector.tensor_tensor(out=into[:, s, :].rearrange("q (t p) -> q t p", p=P), in0=rows, in1=acc, op=SUBTRACT)
+        def subtract2(n, s, t0, t1, x2):
+            gated = running[n][:, s, :].rearrange("p (t r) -> p t r", t=PACK)[:, t0:t1]
+            product = c2[n, s][:].rearrange("p (r t) -> p t r", t=PACK)[:, t0:t1]
+            nc.vector.tensor_tensor(out=x2[:, s, :].rearrange("p (t r) -> p t r", r=P), in0=gated, in1=product, op=SUBTRACT)
 
-        def weave_x2(copy, x2):
-            woven = sbuf("wide", 5, [P, PACK * x2.shape[2]], BF16)
-            copy(
-                out=woven[:].rearrange("p (c i s) -> p c s i", i=4, s=PACK),
-                in_=x2[:].rearrange("p s (c i) -> p c s i", i=4),
-            )
+        def x2_woven_like(x2):
+            return sbuf("wide", WIDE_BUFS, [P, PACK * x2.shape[2]], BF16)
+
+        def weave_x2(x2):
+            woven = x2_woven_like(x2)
+            weave_by_copy(nc.scalar.copy, woven[:], x2[:])
             return woven
 
-        def weave_x2_pool(x2):
-            woven = sbuf("wide", 5, [P, PACK * x2.shape[2]], BF16)
-            nc.gpsimd.tensor_scalar(
-                out=woven[:].rearrange("p (c s) -> p c s", s=PACK),
-                in0=x2[:].rearrange("p s c -> p c s"),
-                scalar1=1.0,
-                scalar2=0.0,
-                op0=MULT,
-                op1=ADD,
-            )
-            return woven
+        def quantise_x2(woven):
+            return quantise(woven[:], "x2", 2)
 
-        def project3(n, s, b):
-            acc3[n, s] = bank(b)[:]
-            mx_pass(acc3[n, s], p3q, s, x2q[n], 0, True, True)
+        def project3(n, s):
+            c3[n, s] = bank(Y_BANKS[s])[:]
+            mx_pass(c3[n, s], p3_mx, s, x2_mx[n], 0, True, True)
 
-        def gate3(n, s, x2, acc, lo, hi):
+        def gate3(n, s, x2, product, lo, hi):
             if lo == 0:
-                yt[n, s] = sbuf("half", 8, [P, W], F32)
+                y_turned[n, s] = sbuf("half", HALF_BUFS, [P, W], F32)
             nc.vector.scalar_tensor_tensor(
-                out=yt[n, s][:, lo:hi], in0=x2, scalar=g3_sb[:, s : s + 1], in1=acc, op0=MULT, op1=SUBTRACT
+                out=y_turned[n, s][:, lo:hi], in0=x2, scalar=g3_sb[:, s : s + 1], in1=product, op0=MULT, op1=SUBTRACT
             )
+
+        def gate3_whole(n):
+            for s in range(PACK):
+                gate3(n, s, running[n][:, s, :], c3[n, s], 0, W)
 
         def turn_y(n, t, b):
-            turned[n, t] = bank(b)
+            y_bank[n, t] = bank(b)
             for s in range(PACK):
-                nc.tensor.transpose(turned[n, t][:, P * s : P * (s + 1)], yt[n, s][:, P * t : P * (t + 1)], ident[:])
+                nc.tensor.transpose(y_bank[n, t][:, P * s : P * (s + 1)], y_turned[n, s][:, P * t : P * (t + 1)], ident[:])
 
-        def store_y(n, t, copy):
+        def store_y(n, t, copy, alone):
             if t % 2 == 0:
-                y_rows[n, t // 2] = sbuf("raw", 7, [P, 2, W], F32)
+                y_rows[n, t // 2] = sbuf("raw", RAW_BUFS, [P, 2, W], F32)
             rows = y_rows[n, t // 2]
-            copy(out=rows[:, t % 2, :].rearrange("p (f s) -> p f s", s=PACK), in_=turned[n, t][:].rearrange("p (s f) -> p f s", s=PACK))
-            if n == GROUPS - 1:
+            copy(
+                out=rows[:, t % 2, :].rearrange("r (p s) -> r p s", s=PACK),
+                in_=y_bank[n, t][:].rearrange("r (s p) -> r p s", s=PACK),
+            )
+            if alone:
                 nc.sync.dma_start(out=out_rows[n, :, t, :], in_=rows[:, t % 2, :])
             elif t % 2:
                 nc.sync.dma_start(out=out_rows[n, :, t - 1 : t + 1, :], in_=rows[:])
 
+        def turn_and_store_y(n, token_slots, banks):
+            for t, b in zip(token_slots, banks):
+                turn_y(n, t, b)
+                store_y(n, t, nc.scalar.copy, False)
+
         def warm_up(count, b):
-            bk = bank(b)
-            for i in range(count):
-                mx_pass(bk[:, :P], ones_q, 0, ones_q, 0, True, True)
+            scratch = bank(b)
+            for repeat in range(count):
+                mx_pass(scratch[:, :P], ones_mx, 0, ones_mx, 0, True, True)
+
+        slots = range(PACK)
 
         ones = sbuf("ones", 1, [P, W], BF16)
         nc.vector.memset(ones[:], 1.0)
-        ones_q = quantise(ones[:], "ones", 1)
-        warm_up(WARM_FIRST, 7)
-        turn_x(0, 0, 0)
-        warm_up(WARM_NEXT, 7)
-        p1g = sbuf("x1b", 2, [P, PACK * W], BF16)
-        regroup_weight(nc.vector.tensor_copy, p1g, "p1", 0)
-        regroup_weight(nc.vector.tensor_copy, p1g, "p1", 1)
-        early = quantise(xt[0][:, : PACK * HALF], "x", 3)
-        p1q = quantise(p1g[:], "p1", 1)
-        turn_x(0, 1, 1)
-        turn_x(1, 0, 0)
-        turn_x(1, 1, 5)
-        p3g = sbuf("stage_first", 1, [P, PACK * W], BF16)
-        regroup_weight(nc.scalar.copy, p3g, "p3", 0)
-        regroup_weight(nc.scalar.copy, p3g, "p3", 1)
-        acc_early = {}
-        acc_late = {}
-        project_half(acc_early, p1q, early, MM_BANKS[:2])
-        late = quantise(xt[0][:, PACK * HALF :], "x", 3)
-        project_half(acc_late, p1q, late, MM_BANKS[2:])
-        for s in range(PACK):
-            gate1(0, s, acc_early[s], 0, HALF)
-        xq[1] = quantise(xt[1][:], "x", 3)
+        ones_mx = quantise(ones[:], "ones", 1)
+        warm_up(WARM_AT_START, G2_BANK)
+        turn_x(0, 0, TURN_BANKS[0])
+        warm_up(WARM_IN_GAP, G2_BANK)
+        p1_woven = sbuf("x1_woven", 2, [P, PACK * W], BF16)
+        weave_weight(nc.vector.tensor_copy, p1_woven, "p1", 0)
+        weave_weight(nc.vector.tensor_copy, p1_woven, "p1", 1)
+        x_first_mx = quantise(x_woven[0][:, : PACK * HALF], "x", 3)
+        p1_mx = quantise(p1_woven[:], "p1", 1)
+        turn_x(0, 1, TURN_BANKS[1])
+        turn_x(1, 0, TURN_BANKS[0])
+        turn_x(1, 1, TURN_BANKS[2])
+        p3_woven = sbuf("first_batch", 1, [P, PACK * W], BF16)
+        weave_weight(nc.scalar.copy, p3_woven, "p3", 0)
+        weave_weight(nc.scalar.copy, p3_woven, "p3", 1)
+        c1_first = project_half(p1_mx, x_first_mx, 0, EARLY_BANKS[:2])
+        x_second_mx = quantise(x_woven[0][:, PACK * HALF :], "x", 3)
+        c1_second = project_half(p1_mx, x_second_mx, 0, EARLY_BANKS[2:])
+        for s in slots:
+            gate1(0, s, c1_first[s], 0, HALF)
+        quantise_x(1)
         project1(1, 0)
         project1(1, 1)
-        for s in range(PACK):
-            gate1(0, s, acc_late[s], HALF, W)
-        p3q = quantise(p3g[:], "p3", 1)
-        turn_x1(0, 0, 0)
-        turn_x1(0, 1, 1)
+        for s in slots:
+            gate1(0, s, c1_second[s], HALF, W)
+        p3_mx = quantise(p3_woven[:], "p3", 1)
+        turn_x1(0, 0, TURN_BANKS[0])
+        turn_x1(0, 1, TURN_BANKS[1])
         project1(1, 2)
         project1(1, 3)
-        turn_x1(0, 2, 5)
-        turn_x1(0, 3, 0)
+
+        weave_gpsimd_share(0, "first_batch")
+        weave_scalar_share(0)
+        load_p2(1, 1)
+        turn_x1(0, 2, TURN_BANKS[2])
+        turn_x1(0, 3, TURN_BANKS[0])
         spread_g2(0)
+        turn_x(2, 0, TURN_BANKS[1])
+        turn_x(2, 1, TURN_BANKS[2])
+        for s in slots:
+            gate1(1, s, c1[1, s], 0, W)
+        turn_x1(1, 0, TURN_BANKS[0])
+        turn_x1(1, 1, TURN_BANKS[1])
+        gate2(0)
+        quantise_x(2)
+        for s in slots:
+            project1(2, s)
+        spread_g2(1)
+        quantise_batch(0)
+        quantise_x1(0)
 
-        for g in range(1, GROUPS):
-            weave_shared((0, 2, 3)[g - 1], POOL_COLS)
-            if g == 2:
-                weave_scalar(2, POOL_COLS, 2 * W)
-            if g + 1 < GROUPS:
-                turn_x(g + 1, 0, 1)
-                turn_x(g + 1, 1, 5)
-            if g == 2:
-                turn_x1(1, 2, 0)
-                turn_x1(1, 3, 1)
-            for s in range(PACK):
-                gate1(g, s, acc1[g, s], 0, W)
-                if g == 1:
-                    if s < 2:
-                        turn_x1(g, s, s)
-                else:
-                    turn_x1(g, s, (5, 0, 1, 5)[s] if g == GROUPS - 1 else MM_BANKS[s])
-            gate2(g - 1)
-            if g == GROUPS - 1:
-                for s in range(PACK):
-                    project2(0, s, (0, 1))
-            if g < GROUPS - 1:
-                if g == 1:
-                    weave_scalar(0, POOL_COLS, 2 * W)
-                else:
-                    load_p2(1, GROUPS - 1)
-                    for q in range(3):
-                        weave_quarter(1, q)
-                xq[g + 1] = quantise(xt[g + 1][:], "x", 3)
-                for s in range(PACK):
-                    project1(g + 1, s)
-                spread_g2(g)
-            else:
-                weave_quarter(1, 3, nc.vector.tensor_copy)
-                weave_quarter(5, 0)
-                weave_quarter(5, 1)
-            if g < GROUPS - 1:
-                x1q[g - 1] = quantise(x1b[g - 1][:], "x1", 4)
-            if g == 2:
-                quantise_p2(0)
-            if g > 1:
-                x1q[g] = quantise(x1b[g][:], "x1", 4)
-            if g == GROUPS - 1:
-                quantise_p2(1)
-                spread_g2(g)
-                for s in range(PACK):
-                    project2(0, s, (3, 2))
-            if g > 1:
-                quantise_p2(g)
+        weave_gpsimd_share(2, "gpsimd_batch")
+        weave_scalar_share(2)
+        weave_quarter(1, 0, nc.scalar.copy)
+        turn_x(3, 0, TURN_BANKS[1])
+        turn_x(3, 1, TURN_BANKS[2])
+        turn_x1(1, 2, TURN_BANKS[0])
+        turn_x1(1, 3, TURN_BANKS[1])
+        for s in slots:
+            gate1(2, s, c1[2, s], 0, W)
+            turn_x1(2, s, EARLY_BANKS[s])
+        gate2(1)
+        weave_quarter(1, 1, nc.scalar.copy)
+        weave_quarter(1, 2, nc.scalar.copy)
+        quantise_x(3)
+        for s in slots:
+            project1(3, s)
+        spread_g2(2)
+        quantise_x1(1)
+        quantise_batch(2)
 
-        last = GROUPS - 1
-        for n in range(last):
-            if n < 2:
-                weave_shared((4, 6)[n], POOL_COLS)
-            else:
-                tail_stage = sbuf("stage_shared", 1, [P, 2 * PACK * W], BF16)
-                stage[7] = tail_stage
-                weave_pool(7, W, W + HALF)
-                weave_scalar(7, W + HALF, 2 * W)
-            if n == 0:
-                weave_quarter(5, 2)
-            for s in range(PACK):
-                subtract2(n, s, 0, PACK, run[n])
-                if n == 1 and s < 2:
-                    project3(0, s + 2, Y_BANKS[s + 2])
-                else:
-                    project2(n + 1, s, (0, 1, 2, 3) if n < 2 else (0, 1, 2))
-            woven = weave_x2(nc.scalar.copy, run[n])
-            if n == 2:
-                p2q[last, 3] = (quantise(tail_stage[:, PACK * W :], "p2_tail", 2), 0)
-                for s in range(PACK):
-                    project2(last, s, (3,))
-            if n == 0:
-                weave_quarter(7, 0)
-                weave_quarter(7, 1)
-                gate2(last)
-            else:
-                for s in range(PACK):
-                    gate3(n - 1, s, run[n - 1][:, s, :], acc3[n - 1, s], 0, W)
-                for t in range(PACK if n == 1 else 2):
-                    turn_y(n - 1, t, Y_BANKS[t])
-                    store_y(n - 1, t, nc.scalar.copy)
-            if n == 0:
-                weave_quarter(5, 3, nc.vector.tensor_copy)
-            x2q[n] = quantise(woven[:], "x2", 2)
-            if n == 0:
-                quantise_p2(5)
-            if n == 1:
-                p2q[last, 2] = (quantise(stage[7][:, : PACK * W], "p2_tail", 2), 0)
-            if n < 2:
-                quantise_p2((4, 6)[n])
-                for s in range(PACK if n else 2):
-                    project3(n, s, Y_BANKS[s])
-            if n == 0:
-                project2(2, 0, (2, 3))
-                project2(2, 1, (2, 3, 0, 1))
-                project2(2, 0, (0, 1))
+        weave_gpsimd_share(3, "gpsimd_batch")
+        for s, b in zip(slots, (TURN_BANKS[2], TURN_BANKS[0], TURN_BANKS[1], EARLY_BANKS[3])):
+            gate1(3, s, c1[3, s], 0, W)
+            turn_x1(3, s, b)
+        gate2(2)
+        for s in slots:
+            project2(0, s, (0, 1))
+        weave_quarter(1, 3, nc.vector.tensor_copy)
+        weave_scalar_share(3)
+        for q in range(3):
+            weave_quarter(5, q, nc.scalar.copy)
+        quantise_x1(2)
+        quantise_x1(3)
+        quantise_batch(1)
+        spread_g2(3)
+        for s in slots:
+            project2(0, s, (3, 2))
+        quantise_batch(3)
 
-        project_half(acc_early, p3q, x2q[last - 1], Y_BANKS[2:])
-        for t in range(2, PACK):
-            turn_y(last - 2, t, Y_BANKS[t % 2])
-            store_y(last - 2, t, nc.scalar.copy)
-        x2_early = sbuf("wide", 5, [P, PACK, HALF], F32)
-        x2_late = sbuf("wide", 5, [P, PACK, HALF], F32)
-        for s in range(PACK):
-            subtract2(last, s, 0, 2, x2_early)
-        woven_early = weave_x2_pool(x2_early)
-        for s in range(PACK):
-            gate3(last - 1, s, run[last - 1][:, s, :HALF], acc_early[s], 0, HALF)
-        project_half(acc_late, p3q, x2q[last - 1], Y_BANKS[2:], HALF)
-        turn_y(last - 1, 0, Y_BANKS[0])
-        turn_y(last - 1, 1, Y_BANKS[1])
-        store_y(last - 1, 0, nc.scalar.copy)
-        for s in range(PACK):
-            subtract2(last, s, 2, PACK, x2_late)
-        warm_up(WARM_NEXT, LATE_BANKS[0])
-        woven_late = weave_x2(nc.scalar.copy, x2_late)
-        store_y(last - 1, 1, nc.scalar.copy)
-        for s in range(PACK):
-            gate3(last - 1, s, run[last - 1][:, s, HALF:], acc_late[s], HALF, W)
-        for t in range(2, PACK):
-            turn_y(last - 1, t, Y_BANKS[t])
-            store_y(last - 1, t, nc.scalar.copy)
-        early = quantise(woven_early[:], "x2", 2)
-        late = quantise(woven_late[:], "x2", 2)
-        project_half(acc_early, p3q, early, LATE_BANKS[:2])
-        project_half(acc_late, p3q, late, LATE_BANKS[2:])
-        for s in range(PACK):
-            gate3(last, s, x2_early[:, s, :], acc_early[s], 0, HALF)
-        turn_y(last, 0, Y_BANKS[0])
-        turn_y(last, 1, Y_BANKS[1])
-        for s in range(PACK):
-            gate3(last, s, x2_late[:, s, :], acc_late[s], HALF, W)
-        turn_y(last, 2, LATE_BANKS[0])
-        turn_y(last, 3, LATE_BANKS[1])
-        for t in range(PACK):
-            store_y(last, t, nc.vector.tensor_copy if t == 2 else nc.scalar.copy)
+        weave_gpsimd_share(4, "gpsimd_batch")
+        weave_quarter(5, 3, nc.scalar.copy)
+        weave_scalar_share(4)
+        for s in slots:
+            subtract2(0, s, 0, PACK, running[0])
+            project2(1, s, range(GROUPS))
+        x2_woven = weave_x2(running[0])
+        weave_quarter(7, 0, nc.scalar.copy)
+        weave_quarter(7, 1, nc.scalar.copy)
+        gate2(3)
+        quantise_batch(5)
+        project2(2, 0, (2, 3))
+        project2(2, 1, (2, 3))
+        x2_mx[0] = quantise_x2(x2_woven)
+        quantise_batch(4)
+        project3(0, 0)
+        project3(0, 1)
+        project2(2, 0, (0, 1))
+        project2(2, 1, (0, 1))
+
+        weave_gpsimd_share(6, "gpsimd_batch")
+        weave_scalar_share(6)
+        for s in slots:
+            subtract2(1, s, 0, PACK, running[1])
+            if s < 2:
+                project3(0, s + 2)
+            else:
+                project2(2, s, range(GROUPS))
+        x2_woven = weave_x2(running[1])
+        gate3_whole(0)
+        turn_and_store_y(0, slots, Y_BANKS)
+        quantise_chunk(7, 0)
+        x2_mx[1] = quantise_x2(x2_woven)
+        quantise_batch(6)
+        for s in slots:
+            project3(1, s)
+
+        p2_woven[7] = sbuf("gpsimd_batch", 1, [P, 2 * PACK * W], BF16)
+        weave_on_gpsimd(*batch_views(7, W, W + HALF))
+        weave_by_copy(nc.scalar.copy, *batch_views(7, W + HALF, 2 * W))
+        for s in slots:
+            subtract2(2, s, 0, PACK, running[2])
+            project2(LAST, s, range(LAST))
+        x2_woven = weave_x2(running[2])
+        quantise_chunk(7, 1)
+        for s in slots:
+            project2(LAST, s, (LAST,))
+        gate3_whole(1)
+        turn_and_store_y(1, (0, 1), Y_BANKS[:2])
+        x2_mx[2] = quantise_x2(x2_woven)
+
+        c3_first = project_half(p3_mx, x2_mx[2], 0, Y_BANKS[2:])
+        turn_and_store_y(1, (2, 3), Y_BANKS[:2])
+        x2_first = sbuf("wide", WIDE_BUFS, [P, PACK, HALF], F32)
+        x2_second = sbuf("wide", WIDE_BUFS, [P, PACK, HALF], F32)
+        for s in slots:
+            subtract2(LAST, s, 0, 2, x2_first)
+        x2_first_woven = x2_woven_like(x2_first)
+        weave_on_gpsimd(x2_first_woven[:], x2_first[:])
+        for s in slots:
+            gate3(2, s, running[2][:, s, :HALF], c3_first[s], 0, HALF)
+        c3_second = project_half(p3_mx, x2_mx[2], HALF, Y_BANKS[2:])
+        turn_y(2, 0, Y_BANKS[0])
+        turn_y(2, 1, Y_BANKS[1])
+        store_y(2, 0, nc.scalar.copy, True)
+        for s in slots:
+            subtract2(LAST, s, 2, PACK, x2_second)
+        warm_up(WARM_IN_GAP, LATE_BANKS[0])
+        x2_second_woven = weave_x2(x2_second)
+        store_y(2, 1, nc.scalar.copy, True)
+        for s in slots:
+            gate3(2, s, running[2][:, s, HALF:], c3_second[s], HALF, W)
+        turn_and_store_y(2, (2, 3), Y_BANKS[2:])
+        x2_first_mx = quantise_x2(x2_first_woven)
+        x2_second_mx = quantise_x2(x2_second_woven)
+        c3_first = project_half(p3_mx, x2_first_mx, 0, LATE_BANKS[:2])
+        c3_second = project_half(p3_mx, x2_second_mx, 0, LATE_BANKS[2:])
+        for s in slots:
+            gate3(LAST, s, x2_first[:, s, :], c3_first[s], 0, HALF)
+        turn_y(LAST, 0, Y_BANKS[0])
+        turn_y(LAST, 1, Y_BANKS[1])
+        for s in slots:
+            gate3(LAST, s, x2_second[:, s, :], c3_second[s], HALF, W)
+        turn_y(LAST, 2, LATE_BANKS[0])
+        turn_y(LAST, 3, LATE_BANKS[1])
+        store_y(LAST, 0, nc.scalar.copy, True)
+        store_y(LAST, 1, nc.scalar.copy, True)
+        store_y(LAST, 2, nc.vector.tensor_copy, True)
+        store_y(LAST, 3, nc.scalar.copy, True)

from contextlib import ExitStack

import concourse.mybir as mybir
from concourse.masks import make_identity

M, D = 2048, 512
FLOPS = 2 * M * D * D + 2 * M * M * D + 2 * M * D * D

F32 = mybir.dt.float32
BF16 = mybir.dt.bfloat16
U32 = mybir.dt.uint32
U8 = mybir.dt.uint8
FP8X4 = mybir.dt.float8_e4m3fn_x4
MULT = mybir.AluOpType.mult
ADD = mybir.AluOpType.add
SUBTRACT = mybir.AluOpType.subtract

P = 128
PACK = 4
W = 512
HALF = W // 2
GROUPS = M // W
LAST = GROUPS - 1

BATCHES = (
    ((0, 0), (1, 0)),
    ((0, 2), (0, 3)),
    ((0, 1), (1, 1)),
    ((1, 2), (1, 3)),
    ((2, 0), (2, 1)),
    ((2, 2), (2, 3)),
    ((3, 0), (3, 1)),
    ((3, 2), (3, 3)),
)
GPSIMD_COLS = 768
QUARTER = 2 * W // 4
WARM_AT_START = 16
WARM_IN_GAP = 8

EARLY_BANKS = (2, 3, 4, 6)
LATE_BANKS = (1, 7, 4, 6)
Y_BANKS = (5, 0, 2, 3)
TURN_BANKS = (0, 1, 5)
G2_BANK = 7

HALF_BUFS = 8
WIDE_BUFS = 5
RAW_BUFS = 7


def tile_gated_relaxed_block_projections_t1_kernel(tc, x, p1, p2, p3, g1, g2, g3, out):
    nc = tc.nc
    with ExitStack() as ctx:
        sb = ctx.enter_context(tc.tile_pool(name="sb", bufs=1))
        ps = ctx.enter_context(tc.psum_pool(name="ps", bufs=1))
        ctx.enter_context(tc.manual_schedule())

        def sbuf(tag, bufs, shape, dtype):
            return sb.tile(shape, dtype, name=tag, tag=tag, bufs=bufs, align_bytes=64)

        def bank(b):
            return ps.tile([P, W], F32, name="bank%d" % b, tag="bank%d" % b)

        def quantise(woven, tag, bufs):
            words = woven.shape[1] // PACK
            codes = sbuf(tag + "_codes", bufs, [P, words], U32)
            scales = sbuf(tag + "_scales", bufs, [P, words], U8)
            nc.vector.quantize_mx(out=codes[:].bitcast(FP8X4), scales=scales[:], in_=woven)
            return codes, scales

        def mx_pass(acc, stationary, s, moving, first_col, start, stop):
            cols = slice(P * s, P * (s + 1))
            span = slice(first_col, first_col + acc.shape[1])
            nc.tensor.matmul_mx(
                out=acc,
                lhsT=stationary[0][:, cols].bitcast(FP8X4),
                lhsT_scale=stationary[1][:, cols],
                rhs=moving[0][:, span].bitcast(FP8X4),
                rhs_scale=moving[1][:, span],
                start=start,
                stop=stop,
            )

        g1_sb = sbuf("g1", 1, [P, PACK], BF16)
        g3_sb = sbuf("g3", 1, [P, PACK], BF16)
        g2_sb = sbuf("g2", 1, [P, GROUPS, PACK], BF16)
        nc.scalar.dma_start(out=g1_sb[:], in_=g1.rearrange("(p s) -> p s", s=PACK))

        x_rows = x.rearrange("(g r t) d -> g r t d", r=P, t=PACK)
        out_rows = out.rearrange("(g r t) d -> g r t d", r=P, t=PACK)
        x_raw = {}
        raw = {}

        def load_x(g, h):
            x_raw[g, h] = sbuf("half", HALF_BUFS, [P, 2 * D], BF16)
            nc.sync.dma_start(out=x_raw[g, h][:].rearrange("r (t d) -> r t d", t=2), in_=x_rows[g, :, 2 * h : 2 * h + 2, :])

        def load_rows(key, rows, tag, bufs):
            raw[key] = sbuf(tag, bufs, [P, PACK, rows.shape[1]], BF16)
            nc.sync.dma_start(out=raw[key][:], in_=rows.rearrange("(p j) c -> p j c", j=PACK))

        def load_p2(pair, k):
            load_rows((pair, k), p2[W * k : W * (k + 1), 2 * W * pair : 2 * W * (pair + 1)], "raw", RAW_BUFS)

        load_x(0, 0)
        load_rows("p1", p1, "wide", WIDE_BUFS)
        load_x(0, 1)
        load_x(1, 0)
        load_x(1, 1)
        load_rows("p3", p3, "wide", WIDE_BUFS)
        nc.sync.dma_start(out=g2_sb[:], in_=g2.rearrange("(g r t) -> r g t", r=P, t=PACK))
        load_p2(0, 0)
        load_x(2, 0)
        load_x(2, 1)
        load_p2(0, 1)
        load_p2(0, 2)
        load_x(3, 0)
        load_x(3, 1)
        load_p2(0, 3)
        nc.sync.dma_start(out=g3_sb[:], in_=g3.rearrange("(p s) -> p s", s=PACK))
        load_p2(1, 2)
        load_p2(1, 3)
        load_p2(1, 0)

        ident = sbuf("ident", 1, [P, P], F32)
        make_identity(nc, ident[:])

        x_woven = {}
        x_mx = {}
        running = {}
        x1_woven = {}
        x1_mx = {}
        p2_woven = {}
        p2_mx = {}
        x2_mx = {}
        c1 = {}
        c2 = {}
        c2_passes = {}
        c3 = {}
        g2_spread = {}
        y_turned = {}
        y_bank = {}
        y_rows = {}

        def turn_x(g, h, b):
            if h == 0:
                x_woven[g] = sbuf("wide", WIDE_BUFS, [P, PACK * W], BF16)
                running[g] = sbuf("running", GROUPS, [P, PACK, W], F32)
            words = x_raw[g, h][:].bitcast(F32)
            turned = bank(b)
            for t in range(2):
                for u in range(2):
                    row = slice(HALF * t + u, HALF * (t + 1), 2)
                    nc.tensor.transpose(turned[:, P * (2 * t + u) : P * (2 * t + u + 1)], words[:, row], ident[:])
            dst = x_woven[g][:].bitcast(F32)[:, W * h : W * (h + 1)]
            nc.scalar.copy(
                out=dst.rearrange("p (t r u) -> p t r u", t=2, u=2),
                in_=turned[:].rearrange("p (t u r) -> p t r u", t=2, u=2),
            )

        def weave_weight(copy, woven, key, h):
            half = slice(P // 4 * h, P // 4 * (h + 1))
            dst = woven[:].rearrange("p (s a b j) -> p a s b j", s=PACK, b=2, j=PACK)
            src = raw[key][:].rearrange("p j (a b s) -> p a s b j", s=PACK, b=2)
            copy(out=dst[:, half], in_=src[:, half])

        def quantise_x(g):
            x_mx[g] = quantise(x_woven[g][:], "x", 3)

        def project1(g, s):
            c1[g, s] = bank(EARLY_BANKS[s])[:]
            mx_pass(c1[g, s], p1_mx, s, x_mx[g], 0, True, True)

        def project_half(weight_mx, moving, first_col, banks):
            sums = []
            for b in banks:
                both = bank(b)
                for side in range(2):
                    sums.append(both[:, HALF * side : HALF * (side + 1)])
                    mx_pass(sums[-1], weight_mx, len(sums) - 1, moving, first_col, True, True)
            return sums

        def gate1(g, s, product, lo, hi):
            nc.vector.scalar_tensor_tensor(
                out=running[g][:, s, lo:hi],
                in0=x_woven[g][:].rearrange("p (n s) -> p n s", s=PACK)[:, lo:hi, s],
                scalar=g1_sb[:, s : s + 1],
                in1=product,
                op0=MULT,
                op1=SUBTRACT,
            )

        def turn_x1(g, s, b):
            if s == 0 and g == 0:
                x1_woven[g] = sbuf("gpsimd_batch", 1, [P, PACK * W], BF16)
            elif s == 0:
                x1_woven[g] = sbuf("x1_woven", 2, [P, PACK * W], BF16)
            turned = bank(b)
            for t in range(PACK):
                nc.tensor.transpose(turned[:, P * t : P * (t + 1)], running[g][:, s, P * t : P * (t + 1)], ident[:])
            nc.scalar.copy(
                out=x1_woven[g][:, W * s : W * (s + 1)].rearrange("r (p t) -> r p t", t=PACK),
                in_=turned[:].rearrange("r (t p) -> r p t", t=PACK),
            )

        def quantise_x1(g):
            x1_mx[g] = quantise(x1_woven[g][:], "x1", GROUPS)

        def spread_g2(g):
            words = g2_sb[:].rearrange("r g t -> r (g t)").bitcast(F32)
            g2_spread[g] = bank(G2_BANK)
            for u in range(2):
                word = words[:, 2 * g + u : 2 * g + u + 1].to_broadcast([P, P])
                nc.tensor.transpose(g2_spread[g][:, P * u : P * (u + 1)], word, ident[:])

        def gate2(g):
            gates = g2_spread[g][:, :HALF].bitcast(BF16).rearrange("p (u r e) -> p u e r", u=2, e=2)
            for s in range(PACK):
                rows = running[g][:, s, :].rearrange("p (u e r) -> p u e r", u=2, e=2)
                nc.vector.tensor_tensor(out=rows, in0=rows, in1=gates, op=MULT)

        def weave_by_copy(copy, dst, src):
            copy(out=dst.rearrange("p (c i j) -> p c j i", i=4, j=PACK), in_=src.rearrange("p j (c i) -> p c j i", i=4))

        def weave_on_gpsimd(dst, src):
            nc.gpsimd.tensor_scalar(
                out=dst.rearrange("p (c j) -> p c j", j=PACK),
                in0=src.rearrange("p j c -> p c j"),
                scalar1=1.0,
                scalar2=0.0,
                op0=MULT,
                op1=ADD,
            )

        def batch_views(i, lo, hi):
            n, k = BATCHES[i][lo // W]
            first = W * (n % 2) + lo % W
            return p2_woven[i][:, PACK * lo : PACK * hi], raw[n // 2, k][:, :, first : first + hi - lo]

        def weave_gpsimd_share(i, tag):
            p2_woven[i] = sbuf(tag, 1, [P, 2 * PACK * W], BF16)
            weave_on_gpsimd(*batch_views(i, 0, W))
            weave_on_gpsimd(*batch_views(i, W, GPSIMD_COLS))

        def weave_scalar_share(i):
            weave_by_copy(nc.scalar.copy, *batch_views(i, GPSIMD_COLS, 2 * W))

        def weave_quarter(i, q, copy):
            if q == 0:
                p2_woven[i] = sbuf("scalar_batch", 2, [P, 2 * PACK * W], BF16)
            weave_by_copy(copy, *batch_views(i, QUARTER * q, QUARTER * (q + 1)))

        def quantise_batch(i):
            made = quantise(p2_woven[i][:], "p2", len(BATCHES) - 1)
            p2_mx[BATCHES[i][0]] = (made, 0)
            p2_mx[BATCHES[i][1]] = (made, W)

        def quantise_chunk(i, which):
            woven = p2_woven[i][:, PACK * W * which : PACK * W * (which + 1)]
            p2_mx[BATCHES[i][which]] = (quantise(woven, "p2_last", 2), 0)

        def project2(n, s, ks):
            for k in ks:
                done = c2_passes.get((n, s), 0)
                if done == 0:
                    c2[n, s] = bank((EARLY_BANKS if n < 2 else LATE_BANKS)[s])
                c2_passes[n, s] = done + 1
                mx_pass(c2[n, s][:], x1_mx[k], s, p2_mx[n, k][0], p2_mx[n, k][1], done == 0, done == LAST)

        def subtract2(n, s, t0, t1, x2):
            gated = running[n][:, s, :].rearrange("p (t r) -> p t r", t=PACK)[:, t0:t1]
            product = c2[n, s][:].rearrange("p (r t) -> p t r", t=PACK)[:, t0:t1]
            nc.vector.tensor_tensor(out=x2[:, s, :].rearrange("p (t r) -> p t r", r=P), in0=gated, in1=product, op=SUBTRACT)

        def x2_woven_like(x2):
            return sbuf("wide", WIDE_BUFS, [P, PACK * x2.shape[2]], BF16)

        def weave_x2(x2):
            woven = x2_woven_like(x2)
            weave_by_copy(nc.scalar.copy, woven[:], x2[:])
            return woven

        def quantise_x2(woven):
            return quantise(woven[:], "x2", 2)

        def project3(n, s):
            c3[n, s] = bank(Y_BANKS[s])[:]
            mx_pass(c3[n, s], p3_mx, s, x2_mx[n], 0, True, True)

        def gate3(n, s, x2, product, lo, hi):
            if lo == 0:
                y_turned[n, s] = sbuf("half", HALF_BUFS, [P, W], F32)
            nc.vector.scalar_tensor_tensor(
                out=y_turned[n, s][:, lo:hi], in0=x2, scalar=g3_sb[:, s : s + 1], in1=product, op0=MULT, op1=SUBTRACT
            )

        def gate3_whole(n):
            for s in range(PACK):
                gate3(n, s, running[n][:, s, :], c3[n, s], 0, W)

        def turn_y(n, t, b):
            y_bank[n, t] = bank(b)
            for s in range(PACK):
                nc.tensor.transpose(y_bank[n, t][:, P * s : P * (s + 1)], y_turned[n, s][:, P * t : P * (t + 1)], ident[:])

        def store_y(n, t, copy, alone):
            if t % 2 == 0:
                y_rows[n, t // 2] = sbuf("raw", RAW_BUFS, [P, 2, W], F32)
            rows = y_rows[n, t // 2]
            copy(
                out=rows[:, t % 2, :].rearrange("r (p s) -> r p s", s=PACK),
                in_=y_bank[n, t][:].rearrange("r (s p) -> r p s", s=PACK),
            )
            if alone:
                nc.sync.dma_start(out=out_rows[n, :, t, :], in_=rows[:, t % 2, :])
            elif t % 2:
                nc.sync.dma_start(out=out_rows[n, :, t - 1 : t + 1, :], in_=rows[:])

        def turn_and_store_y(n, token_slots, banks):
            for t, b in zip(token_slots, banks):
                turn_y(n, t, b)
                store_y(n, t, nc.scalar.copy, False)

        def warm_up(count, b):
            scratch = bank(b)
            for repeat in range(count):
                mx_pass(scratch[:, :P], ones_mx, 0, ones_mx, 0, True, True)

        slots = range(PACK)

        ones = sbuf("ones", 1, [P, W], BF16)
        nc.vector.memset(ones[:], 1.0)
        ones_mx = quantise(ones[:], "ones", 1)
        warm_up(WARM_AT_START, G2_BANK)
        turn_x(0, 0, TURN_BANKS[0])
        warm_up(WARM_IN_GAP, G2_BANK)
        p1_woven = sbuf("x1_woven", 2, [P, PACK * W], BF16)
        weave_weight(nc.vector.tensor_copy, p1_woven, "p1", 0)
        weave_weight(nc.vector.tensor_copy, p1_woven, "p1", 1)
        x_first_mx = quantise(x_woven[0][:, : PACK * HALF], "x", 3)
        p1_mx = quantise(p1_woven[:], "p1", 1)
        turn_x(0, 1, TURN_BANKS[1])
        turn_x(1, 0, TURN_BANKS[0])
        turn_x(1, 1, TURN_BANKS[2])
        p3_woven = sbuf("first_batch", 1, [P, PACK * W], BF16)
        weave_weight(nc.scalar.copy, p3_woven, "p3", 0)
        weave_weight(nc.scalar.copy, p3_woven, "p3", 1)
        c1_first = project_half(p1_mx, x_first_mx, 0, EARLY_BANKS[:2])
        x_second_mx = quantise(x_woven[0][:, PACK * HALF :], "x", 3)
        c1_second = project_half(p1_mx, x_second_mx, 0, EARLY_BANKS[2:])
        for s in slots:
            gate1(0, s, c1_first[s], 0, HALF)
        quantise_x(1)
        project1(1, 0)
        project1(1, 1)
        for s in slots:
            gate1(0, s, c1_second[s], HALF, W)
        p3_mx = quantise(p3_woven[:], "p3", 1)
        turn_x1(0, 0, TURN_BANKS[0])
        turn_x1(0, 1, TURN_BANKS[1])
        project1(1, 2)
        project1(1, 3)

        weave_gpsimd_share(0, "first_batch")
        weave_scalar_share(0)
        load_p2(1, 1)
        turn_x1(0, 2, TURN_BANKS[2])
        turn_x1(0, 3, TURN_BANKS[0])
        spread_g2(0)
        turn_x(2, 0, TURN_BANKS[1])
        turn_x(2, 1, TURN_BANKS[2])
        for s in slots:
            gate1(1, s, c1[1, s], 0, W)
        turn_x1(1, 0, TURN_BANKS[0])
        turn_x1(1, 1, TURN_BANKS[1])
        gate2(0)
        quantise_x(2)
        for s in slots:
            project1(2, s)
        spread_g2(1)
        quantise_batch(0)
        quantise_x1(0)

        weave_gpsimd_share(2, "gpsimd_batch")
        weave_scalar_share(2)
        weave_quarter(1, 0, nc.scalar.copy)
        turn_x(3, 0, TURN_BANKS[1])
        turn_x(3, 1, TURN_BANKS[2])
        turn_x1(1, 2, TURN_BANKS[0])
        turn_x1(1, 3, TURN_BANKS[1])
        for s in slots:
            gate1(2, s, c1[2, s], 0, W)
            turn_x1(2, s, EARLY_BANKS[s])
        gate2(1)
        weave_quarter(1, 1, nc.scalar.copy)
        weave_quarter(1, 2, nc.scalar.copy)
        quantise_x(3)
        for s in slots:
            project1(3, s)
        spread_g2(2)
        quantise_x1(1)
        quantise_batch(2)

        weave_gpsimd_share(3, "gpsimd_batch")
        for s, b in zip(slots, (TURN_BANKS[2], TURN_BANKS[0], TURN_BANKS[1], EARLY_BANKS[3])):
            gate1(3, s, c1[3, s], 0, W)
            turn_x1(3, s, b)
        gate2(2)
        for s in slots:
            project2(0, s, (0, 1))
        weave_quarter(1, 3, nc.vector.tensor_copy)
        weave_scalar_share(3)
        for q in range(3):
            weave_quarter(5, q, nc.scalar.copy)
        quantise_x1(2)
        quantise_x1(3)
        quantise_batch(1)
        spread_g2(3)
        for s in slots:
            project2(0, s, (3, 2))
        quantise_batch(3)

        weave_gpsimd_share(4, "gpsimd_batch")
        weave_quarter(5, 3, nc.scalar.copy)
        weave_scalar_share(4)
        for s in slots:
            subtract2(0, s, 0, PACK, running[0])
            project2(1, s, range(GROUPS))
        x2_woven = weave_x2(running[0])
        weave_quarter(7, 0, nc.scalar.copy)
        weave_quarter(7, 1, nc.scalar.copy)
        gate2(3)
        quantise_batch(5)
        project2(2, 0, (2, 3))
        project2(2, 1, (2, 3))
        x2_mx[0] = quantise_x2(x2_woven)
        quantise_batch(4)
        project3(0, 0)
        project3(0, 1)
        project2(2, 0, (0, 1))
        project2(2, 1, (0, 1))

        weave_gpsimd_share(6, "gpsimd_batch")
        weave_scalar_share(6)
        for s in slots:
            subtract2(1, s, 0, PACK, running[1])
            if s < 2:
                project3(0, s + 2)
            else:
                project2(2, s, range(GROUPS))
        x2_woven = weave_x2(running[1])
        gate3_whole(0)
        turn_and_store_y(0, slots, Y_BANKS)
        quantise_chunk(7, 0)
        x2_mx[1] = quantise_x2(x2_woven)
        quantise_batch(6)
        for s in slots:
            project3(1, s)

        p2_woven[7] = sbuf("gpsimd_batch", 1, [P, 2 * PACK * W], BF16)
        weave_on_gpsimd(*batch_views(7, W, W + HALF))
        weave_by_copy(nc.scalar.copy, *batch_views(7, W + HALF, 2 * W))
        for s in slots:
            subtract2(2, s, 0, PACK, running[2])
            project2(LAST, s, range(LAST))
        x2_woven = weave_x2(running[2])
        quantise_chunk(7, 1)
        for s in slots:
            project2(LAST, s, (LAST,))
        gate3_whole(1)
        turn_and_store_y(1, (0, 1), Y_BANKS[:2])
        x2_mx[2] = quantise_x2(x2_woven)

        c3_first = project_half(p3_mx, x2_mx[2], 0, Y_BANKS[2:])
        turn_and_store_y(1, (2, 3), Y_BANKS[:2])
        x2_first = sbuf("wide", WIDE_BUFS, [P, PACK, HALF], F32)
        x2_second = sbuf("wide", WIDE_BUFS, [P, PACK, HALF], F32)
        for s in slots:
            subtract2(LAST, s, 0, 2, x2_first)
        x2_first_woven = x2_woven_like(x2_first)
        weave_on_gpsimd(x2_first_woven[:], x2_first[:])
        for s in slots:
            gate3(2, s, running[2][:, s, :HALF], c3_first[s], 0, HALF)
        c3_second = project_half(p3_mx, x2_mx[2], HALF, Y_BANKS[2:])
        turn_y(2, 0, Y_BANKS[0])
        turn_y(2, 1, Y_BANKS[1])
        store_y(2, 0, nc.scalar.copy, True)
        for s in slots:
            subtract2(LAST, s, 2, PACK, x2_second)
        warm_up(WARM_IN_GAP, LATE_BANKS[0])
        x2_second_woven = weave_x2(x2_second)
        store_y(2, 1, nc.scalar.copy, True)
        for s in slots:
            gate3(2, s, running[2][:, s, HALF:], c3_second[s], HALF, W)
        turn_and_store_y(2, (2, 3), Y_BANKS[2:])
        x2_first_mx = quantise_x2(x2_first_woven)
        x2_second_mx = quantise_x2(x2_second_woven)
        c3_first = project_half(p3_mx, x2_first_mx, 0, LATE_BANKS[:2])
        c3_second = project_half(p3_mx, x2_second_mx, 0, LATE_BANKS[2:])
        for s in slots:
            gate3(LAST, s, x2_first[:, s, :], c3_first[s], 0, HALF)
        turn_y(LAST, 0, Y_BANKS[0])
        turn_y(LAST, 1, Y_BANKS[1])
        for s in slots:
            gate3(LAST, s, x2_second[:, s, :], c3_second[s], HALF, W)
        turn_y(LAST, 2, LATE_BANKS[0])
        turn_y(LAST, 3, LATE_BANKS[1])
        store_y(LAST, 0, nc.scalar.copy, True)
        store_y(LAST, 1, nc.scalar.copy, True)
        store_y(LAST, 2, nc.vector.tensor_copy, True)
        store_y(LAST, 3, nc.scalar.copy, True)
